import numpy as np
import ml_dtypes


def mxq(x, axis, fmt="e4m3"):
    dtype, down = {"e4m3": (ml_dtypes.float8_e4m3fn, 7), "e5m2": (ml_dtypes.float8_e5m2, 14)}[fmt]
    v = np.moveaxis(np.asarray(x, np.float32).astype(ml_dtypes.bfloat16).astype(np.float64), axis, -1)
    blocks = v.reshape(v.shape[:-1] + (-1, 32))
    amax = np.abs(blocks).max(-1, keepdims=True)
    byte = np.maximum(np.where(amax > 0, np.frexp(amax)[1] - 1 + 127, 0) - down, 1)
    scale = np.exp2(byte - 127.0)
    codes = (blocks / scale).astype(np.float32).astype(dtype).astype(np.float64)
    return np.moveaxis((codes * scale).reshape(v.shape), -1, axis)


WIDE = False


def mx_kscale(k):
    if not WIDE:
        return np.ones(k)
    levels = np.array([10, -10, 5, -5, 0])
    if k % 512:
        return np.exp2(np.random.permutation(np.resize(levels, k // 32))).repeat(32)
    a = np.empty((k // 512, 16))
    for p in range(k // 512):
        a[p, :8] = np.random.permutation(np.resize(levels, 8))
        for g in range(8):
            far = levels[np.abs(levels - a[p, g]) >= 10]
            a[p, g + 8] = far[np.random.randint(len(far))]
    return np.exp2(a.ravel()).repeat(32)


def f64(x):
    return np.asarray(x).astype(np.float64)


E2M1 = np.array([0.0, 0.5, 1.0, 1.5, 2.0, 3.0, 4.0, 6.0, -0.0, -0.5, -1.0, -1.5, -2.0, -3.0, -4.0, -6.0])


def pack_weight(w, fmt):
    k, n = w.shape
    w = f64(np.asarray(w, np.float32).astype(ml_dtypes.bfloat16)).reshape(k // 32, 32, n)
    amax = np.abs(w).max(1)
    if fmt == "e4m3":
        byte = np.frexp(amax)[1] - 1 + 127 - 7
    else:
        mant, ex = np.frexp(amax / 6.0)
        byte = np.where(mant > 0.5, ex, ex - 1) + 127
    byte = np.clip(np.where(amax > 0, byte, 1), 1, 254)
    scaled = (w * np.exp2(127.0 - byte)[:, None, :]).reshape(k, n).astype(np.float32)
    by_word = np.ascontiguousarray(scaled.reshape(k // 512, 128, 4, n).transpose(0, 1, 3, 2))
    if fmt == "e4m3":
        words = by_word.astype(ml_dtypes.float8_e4m3fn).view(np.uint8)
    else:
        c = by_word.astype(ml_dtypes.float4_e2m1fn).view(np.uint8) & 0xF
        words = (c[..., 0::2] | (c[..., 1::2] << 4)).reshape(k // 512, 128, 2 * n)
    return np.ascontiguousarray(words), np.ascontiguousarray(byte.astype(np.uint8).reshape(k // 512, 16, n))


def unpack_weight(words, scales, fmt):
    g, _, n = scales.shape
    words = np.ascontiguousarray(words).reshape(g, 128, n, -1)
    if fmt == "e4m3":
        vals = words.view(ml_dtypes.float8_e4m3fn).astype(np.float64)
    else:
        nib = np.empty((g, 128, n, 4), np.uint8)
        nib[..., 0::2] = words & 0xF
        nib[..., 1::2] = words >> 4
        vals = E2M1[nib]
    vals = vals * np.repeat(np.exp2(scales.astype(np.float64) - 127.0), 8, axis=1)[..., None]
    return vals.transpose(0, 1, 3, 2).reshape(g * 512, n)


def planes(y):
    n, m = y.shape
    v = y.astype(np.float32).astype(ml_dtypes.bfloat16).astype(np.float64).reshape(n // 32, 32, m)
    top = np.abs(v).max(1)
    byte = np.clip(np.where(top > 0, np.frexp(top)[1] - 1 + 127 - 7, 1), 1, 254)
    codes = (v * np.exp2(127.0 - byte)[:, None, :]).reshape(n, m).astype(np.float32).astype(ml_dtypes.float8_e4m3fn).view(np.uint8)
    words = codes.reshape(n // 512, 128, 4, m).transpose(0, 1, 3, 2)
    return np.ascontiguousarray(words), np.ascontiguousarray(byte.astype(np.uint8).reshape(n // 512, 16, m))


def gelu(v):
    return 0.5 * v * (1.0 + np.tanh(np.sqrt(2.0 / np.pi) * (v + 0.044715 * v**3)))


K, R, M, T = 1024, 512, 2048, 512


def setup_inputs():
    n = np.random.standard_normal
    s = mx_kscale(K)[:, None]
    u = mx_kscale(R)[:, None]
    p_w4 = pack_weight(n((K, M)) / np.sqrt(K) / s, "e2m1")
    return {
        "x": (n((K, T)) * s).astype(np.float32),
        "w4_words": p_w4[0],
        "w4_scales": p_w4[1],
        "down": (n((K, R)) / np.sqrt(K) / s * u.T).astype(np.float32),
        "up": (0.5 * n((R, M)) / np.sqrt(R) / u).astype(np.float32),
        "b": (0.3 * n(2048)).astype(np.float32),
    }


def reference(x, w4_words, w4_scales, down, up, b):
    x_ = mxq(f64(x), 0, "e4m3")
    w4_ = unpack_weight(w4_words, w4_scales, "e2m1")
    down_ = mxq(f64(down), 0, "e4m3")
    up_ = mxq(f64(up), 0, "e4m3")
    h_ = mxq(down_.T @ x_, 0, "e4m3")
    y = w4_.T @ x_ + up_.T @ h_
    out_0 = gelu(y + f64(b)[:, None])
    return (out_0,) + planes(out_0)

@@ -1,0 +1,259 @@
+from contextlib import ExitStack
+
+import concourse.mybir as mybir
+
+K, R, M, T = 1024, 512, 2048, 512
+FLOPS = 2 * T * (K * R + K * M + R * M)
+
+F32 = mybir.dt.float32
+BF16 = mybir.dt.bfloat16
+I32 = mybir.dt.int32
+U32 = mybir.dt.uint32
+U8 = mybir.dt.uint8
+FP8X4 = mybir.dt.float8_e4m3fn_x4
+FP4X4 = mybir.dt.float4_e2m1fn_x4
+GELU = mybir.ActivationFunctionType.Gelu_apprx_tanh
+
+P = 128
+PACK = 4
+SPAN = P * PACK
+K_PASSES = K // SPAN
+GROUPS = M // SPAN
+TILES = M // P
+BANKS = 8
+HALF = SPAN // 2
+
+
+def tile_mix_lowrank_fm_pl_gelu_kernel(
+    tc, x, w4_words, w4_scales, down, up, b, out_0, out_1, out_2
+):
+    nc = tc.nc
+    with ExitStack() as ctx:
+        sb = ctx.enter_context(tc.tile_pool(name="sb", bufs=1))
+        ps = ctx.enter_context(tc.psum_pool(name="ps", bufs=1))
+        ctx.enter_context(tc.manual_schedule())
+
+        def sbuf(name, shape, dtype):
+            return sb.tile(shape, dtype, name=name, align_bytes=64)
+
+        def load_rows(name, src, cols):
+            width = cols.stop - cols.start
+            raw = sbuf(name, [P, PACK, width], F32)
+            nc.sync.dma_start(out=raw[:], in_=src[:, cols].rearrange("(p j) c -> p j c", j=PACK))
+            return raw
+
+        def copy(engine, out, in_):
+            if engine == "scalar":
+                nc.scalar.copy(out=out, in_=in_)
+            else:
+                nc.vector.tensor_copy(out=out, in_=in_)
+
+        def round_plain(engine, dst, raw, first):
+            width = raw.shape[2]
+            copy(
+                engine,
+                dst[:, first : first + width, :].rearrange("p (c i) j -> p c j i", i=PACK),
+                raw.rearrange("p j (c i) -> p c j i", i=PACK),
+            )
+
+        def round_dealt(engine, dst, raw, first):
+            words = raw.shape[2] // PACK
+            m0 = first // PACK
+            view = dst[:].rearrange("p (s m) j -> p m j s", s=PACK)
+            copy(engine, view[:, m0 : m0 + words, :, :], raw.rearrange("p j (m s) -> p m j s", s=PACK))
+
+        def quantise(codes, scales, grouped):
+            nc.vector.quantize_mx(
+                out=codes.bitcast(FP8X4), scales=scales, in_=grouped[:].rearrange("p c j -> p (c j)")
+            )
+
+        def operand(name):
+            grouped = sbuf(name + "_bf", [P, SPAN, PACK], BF16)
+            codes = sbuf(name + "_codes", [P, SPAN], U32)
+            scales = sbuf(name + "_scales", [P, SPAN], U8)
+            return grouped, codes, scales
+
+        halves = [slice(0, HALF), slice(HALF, SPAN)]
+        x_rows = [x[a * SPAN : (a + 1) * SPAN, :] for a in range(K_PASSES)]
+        down_rows = [down[a * SPAN : (a + 1) * SPAN, :] for a in range(K_PASSES)]
+
+        ws_raw = sbuf("ws_raw", [P, K_PASSES, M], U8)
+        nc.vector.memset(ws_raw[:].rearrange("p a n -> p (a n)").bitcast(I32), 0)
+
+        def load_w4(a):
+            raw = sbuf("w4_raw%d" % a, [P, 2 * M], U8)
+            nc.sync.dma_start(out=raw[:].bitcast(I32), in_=w4_words[a].bitcast(I32))
+            return raw
+
+        x_raw = [[load_rows("x_raw0%d" % h, x_rows[0], halves[h]) for h in range(2)]]
+        for q in range(4):
+            nc.sync.dma_start(
+                out=ws_raw[32 * q : 32 * q + 4, :, :].bitcast(I32),
+                in_=w4_scales[:, 4 * q : 4 * q + 4, :].rearrange("a r n -> r a n").bitcast(I32),
+            )
+        w4_raw = [load_w4(0)]
+        down_raw = [[load_rows("down_raw0%d" % h, down_rows[0], halves[h]) for h in range(2)]]
+        w4_raw.append(load_w4(1))
+        x_raw.append([load_rows("x_raw1%d" % h, x_rows[1], halves[h]) for h in range(2)])
+        down_raw.append([load_rows("down_raw1%d" % h, down_rows[1], halves[h]) for h in range(2)])
+        bias = sbuf("bias", [P, GROUPS, PACK], F32)
+        nc.sync.dma_start(out=bias[:], in_=b.rearrange("(g p j) -> p g j", g=GROUPS, j=PACK))
+        up_raw = [load_rows("up_raw%d" % g, up, slice(g * SPAN, (g + 1) * SPAN)) for g in range(GROUPS)]
+
+        xq = [operand("x%d" % a) for a in range(K_PASSES)]
+        dq = [operand("down%d" % a) for a in range(K_PASSES)]
+        uq = [operand("up%d" % g) for g in range(GROUPS)]
+        hq = operand("h")
+        ws = sbuf("ws", [P, K_PASSES, M], U8)
+        w4 = [sbuf("w4_%d" % a, [P, 2 * M], U8) for a in range(K_PASSES)]
+
+        def deal_w4(a):
+            nc.vector.tensor_copy(
+                out=w4[a][:].rearrange("p (g s m e) -> p g s m e", g=GROUPS, s=PACK, e=2),
+                in_=w4_raw[a][:].rearrange("p (g m s e) -> p g s m e", g=GROUPS, s=PACK, e=2),
+            )
+
+        def deal_ws():
+            nc.vector.tensor_copy(
+                out=ws[:].rearrange("p a (g s m) -> p (a g) s m", g=GROUPS, s=PACK),
+                in_=ws_raw[:].rearrange("p a (g m s) -> p (a g) s m", g=GROUPS, s=PACK),
+            )
+
+        def bank(i, shape):
+            return ps.tile(shape, F32, name="bank%d" % (i % BANKS))
+
+        h_ps = [bank(GROUPS + tb, [P, PACK, P]) for tb in range(PACK)]
+
+        def h_pass(a, tb):
+            t_cols = slice(tb * P, (tb + 1) * P)
+            for j in range(PACK):
+                r_cols = slice(j * P, (j + 1) * P)
+                nc.tensor.matmul_mx(
+                    out=h_ps[tb][:, j, :],
+                    lhsT=dq[a][1][:, r_cols].bitcast(FP8X4),
+                    lhsT_scale=dq[a][2][:, r_cols],
+                    rhs=xq[a][1][:, t_cols].bitcast(FP8X4),
+                    rhs_scale=xq[a][2][:, t_cols],
+                    start=(a == 0 and j == 0),
+                    stop=(a == K_PASSES - 1 and j == PACK - 1),
+                )
+
+        y_ps = {}
+
+        def base_pass(i, a):
+            if a == 0:
+                y_ps[i] = bank(i, [P, T])
+            nc.tensor.matmul_mx(
+                out=y_ps[i][:],
+                lhsT=w4[a][:, 2 * P * i : 2 * P * (i + 1)].bitcast(FP4X4),
+                lhsT_scale=ws[:, a, P * i : P * (i + 1)],
+                rhs=xq[a][1][:].bitcast(FP8X4),
+                rhs_scale=xq[a][2][:],
+                start=(a == 0),
+                stop=False,
+            )
+
+        result = [sbuf("result%d" % g, [P, PACK, T], F32) for g in range(GROUPS)]
+        res_bf = [sbuf("res_bf%d" % g, [P, T, PACK], BF16) for g in range(GROUPS)]
+        res_codes = [sbuf("res_codes%d" % g, [P, T], U32) for g in range(GROUPS)]
+        res_scales = sbuf("res_scales", [P, T], U8)
+
+        def finish_tile(i):
+            g, j = divmod(i, PACK)
+            cols = slice(j * P, (j + 1) * P)
+            nc.tensor.matmul_mx(
+                out=y_ps[i][:],
+                lhsT=uq[g][1][:, cols].bitcast(FP8X4),
+                lhsT_scale=uq[g][2][:, cols],
+                rhs=hq[1][:].bitcast(FP8X4),
+                rhs_scale=hq[2][:],
+                start=False,
+                stop=True,
+            )
+            nc.scalar.activation(out=result[g][:, j, :], in_=y_ps[i][:], func=GELU, bias=bias[:, g, j : j + 1])
+
+        def store_result(g, jh):
+            rows = out_0[g * SPAN : (g + 1) * SPAN, :].rearrange("(p j) t -> p j t", j=PACK)
+            nc.sync.dma_start(out=rows[:, 2 * jh : 2 * jh + 2, :], in_=result[g][:, 2 * jh : 2 * jh + 2, :])
+
+        def quantise_result(g):
+            quantise(res_codes[g][:], res_scales[PACK * g : P, :], res_bf[g])
+
+        def store_words(g):
+            nc.sync.dma_start(
+                out=out_1[g].rearrange("p t i -> p (t i)").bitcast(I32), in_=res_codes[g][:].bitcast(I32)
+            )
+
+        def q(op):
+            quantise(op[1][:], op[2][:], op[0])
+
+        round_plain("scalar", xq[0][0], x_raw[0][0][:], 0)
+        round_plain("vector", xq[0][0], x_raw[0][1][:], HALF)
+        q(xq[0])
+        deal_ws()
+        deal_w4(0)
+        for h in range(2):
+            round_dealt("scalar", dq[0][0], down_raw[0][h][:], h * HALF)
+        q(dq[0])
+        for tb in range(PACK):
+            h_pass(0, tb)
+        for i in range(PACK):
+            base_pass(i, 0)
+        deal_w4(1)
+        for h in range(2):
+            round_plain("scalar", xq[1][0], x_raw[1][h][:], h * HALF)
+        q(xq[1])
+        for i in range(PACK):
+            base_pass(i, 1)
+        round_dealt("scalar", dq[1][0], down_raw[1][0][:], 0)
+        round_dealt("vector", dq[1][0], down_raw[1][1][:], HALF)
+        q(dq[1])
+        for tb in range(PACK):
+            h_pass(1, tb)
+            nc.scalar.copy(out=hq[0][:, tb * P : (tb + 1) * P, :], in_=h_ps[tb][:].rearrange("p j t -> p t j"))
+        round_dealt("vector", uq[0][0], up_raw[0][:], 0)
+        q(uq[0])
+        q(hq)
+        for i in range(PACK, BANKS):
+            for a in range(K_PASSES):
+                base_pass(i, a)
+
+        lag = 2
+        for i in range(TILES):
+            g, j = divmod(i, PACK)
+            if j == 0 and g == 0:
+                round_dealt("vector", uq[1][0], up_raw[1][:], 0)
+                q(uq[1])
+                round_dealt("vector", uq[2][0], up_raw[2][:], 0)
+                q(uq[2])
+                round_dealt("vector", uq[3][0], up_raw[3][:], 0)
+            if i == PACK:
+                round_plain("vector", res_bf[0], result[0][:], 0)
+                q(uq[3])
+                quantise_result(0)
+            finish_tile(i)
+            nxt = i + BANKS - lag
+            if BANKS <= nxt < TILES:
+                for a in range(K_PASSES):
+                    base_pass(nxt, a)
+            if j % 2 == 1:
+                store_result(g, j // 2)
+            if i == 7:
+                store_words(0)
+                round_plain("vector", res_bf[1], result[1][:], 0)
+            if i == 11:
+                round_plain("vector", res_bf[2], result[2][:], 0)
+                quantise_result(1)
+                quantise_result(2)
+            if i == 13:
+                store_words(1)
+        store_words(2)
+        round_plain("vector", res_bf[3], result[3][:, :, 0:352], 0)
+        round_plain("scalar", res_bf[3], result[3][:, :, 352:T], 352)
+        quantise_result(3)
+        store_words(3)
+        for q4 in range(4):
+            nc.sync.dma_start(
+                out=out_2[:, 4 * q4 : 4 * q4 + 4, :].bitcast(I32),
+                in_=res_scales[32 * q4 : 32 * q4 + 16, :].bitcast(I32),
+            )

@@ -22,6 +22,7 @@ GROUPS = M // SPAN
 TILES = M // P
 BANKS = 8
 HALF = SPAN // 2
+VECTOR_SHARE = 352
 
 
 def tile_mix_lowrank_fm_pl_gelu_kernel(
@@ -62,6 +63,10 @@ def tile_mix_lowrank_fm_pl_gelu_kernel(
             view = dst[:].rearrange("p (s m) j -> p m j s", s=PACK)
             copy(engine, view[:, m0 : m0 + words, :, :], raw.rearrange("p j (m s) -> p m j s", s=PACK))
 
+        def round_shared(rounder, dst, raw, split):
+            rounder("scalar", dst, raw[:, :, split:SPAN], split)
+            rounder("vector", dst, raw[:, :, 0:split], 0)
+
         def quantise(codes, scales, grouped):
             nc.vector.quantize_mx(
                 out=codes.bitcast(FP8X4), scales=scales, in_=grouped[:].rearrange("p c j -> p (c j)")
@@ -73,7 +78,6 @@ def tile_mix_lowrank_fm_pl_gelu_kernel(
             scales = sbuf(name + "_scales", [P, SPAN], U8)
             return grouped, codes, scales
 
-        halves = [slice(0, HALF), slice(HALF, SPAN)]
         x_rows = [x[a * SPAN : (a + 1) * SPAN, :] for a in range(K_PASSES)]
         down_rows = [down[a * SPAN : (a + 1) * SPAN, :] for a in range(K_PASSES)]
 
@@ -85,17 +89,18 @@ def tile_mix_lowrank_fm_pl_gelu_kernel(
             nc.sync.dma_start(out=raw[:].bitcast(I32), in_=w4_words[a].bitcast(I32))
             return raw
 
-        x_raw = [[load_rows("x_raw0%d" % h, x_rows[0], halves[h]) for h in range(2)]]
+        whole = slice(0, SPAN)
+        w4_raw = [load_w4(0)]
+        x_raw = [load_rows("x_raw0", x_rows[0], whole)]
         for q in range(4):
             nc.sync.dma_start(
                 out=ws_raw[32 * q : 32 * q + 4, :, :].bitcast(I32),
                 in_=w4_scales[:, 4 * q : 4 * q + 4, :].rearrange("a r n -> r a n").bitcast(I32),
             )
-        w4_raw = [load_w4(0)]
-        down_raw = [[load_rows("down_raw0%d" % h, down_rows[0], halves[h]) for h in range(2)]]
+        down_raw = [load_rows("down_raw0", down_rows[0], whole)]
         w4_raw.append(load_w4(1))
-        x_raw.append([load_rows("x_raw1%d" % h, x_rows[1], halves[h]) for h in range(2)])
-        down_raw.append([load_rows("down_raw1%d" % h, down_rows[1], halves[h]) for h in range(2)])
+        x_raw.append(load_rows("x_raw1", x_rows[1], whole))
+        down_raw.append(load_rows("down_raw1", down_rows[1], whole))
         bias = sbuf("bias", [P, GROUPS, PACK], F32)
         nc.sync.dma_start(out=bias[:], in_=b.rearrange("(g p j) -> p g j", g=GROUPS, j=PACK))
         up_raw = [load_rows("up_raw%d" % g, up, slice(g * SPAN, (g + 1) * SPAN)) for g in range(GROUPS)]
@@ -172,9 +177,9 @@ def tile_mix_lowrank_fm_pl_gelu_kernel(
             )
             nc.scalar.activation(out=result[g][:, j, :], in_=y_ps[i][:], func=GELU, bias=bias[:, g, j : j + 1])
 
-        def store_result(g, jh):
+        def store_result(g, slots):
             rows = out_0[g * SPAN : (g + 1) * SPAN, :].rearrange("(p j) t -> p j t", j=PACK)
-            nc.sync.dma_start(out=rows[:, 2 * jh : 2 * jh + 2, :], in_=result[g][:, 2 * jh : 2 * jh + 2, :])
+            nc.sync.dma_start(out=rows[:, slots, :], in_=result[g][:, slots, :])
 
         def quantise_result(g):
             quantise(res_codes[g][:], res_scales[PACK * g : P, :], res_bf[g])
@@ -187,26 +192,22 @@ def tile_mix_lowrank_fm_pl_gelu_kernel(
         def q(op):
             quantise(op[1][:], op[2][:], op[0])
 
-        round_plain("scalar", xq[0][0], x_raw[0][0][:], 0)
-        round_plain("vector", xq[0][0], x_raw[0][1][:], HALF)
+        deal_w4(0)
+        round_shared(round_plain, xq[0][0], x_raw[0], VECTOR_SHARE)
         q(xq[0])
         deal_ws()
-        deal_w4(0)
-        for h in range(2):
-            round_dealt("scalar", dq[0][0], down_raw[0][h][:], h * HALF)
+        round_dealt("scalar", dq[0][0], down_raw[0][:], 0)
+        deal_w4(1)
         q(dq[0])
         for tb in range(PACK):
             h_pass(0, tb)
         for i in range(PACK):
             base_pass(i, 0)
-        deal_w4(1)
-        for h in range(2):
-            round_plain("scalar", xq[1][0], x_raw[1][h][:], h * HALF)
+        round_shared(round_plain, xq[1][0], x_raw[1], HALF)
         q(xq[1])
         for i in range(PACK):
             base_pass(i, 1)
-        round_dealt("scalar", dq[1][0], down_raw[1][0][:], 0)
-        round_dealt("vector", dq[1][0], down_raw[1][1][:], HALF)
+        round_shared(round_dealt, dq[1][0], down_raw[1], VECTOR_SHARE)
         q(dq[1])
         for tb in range(PACK):
             h_pass(1, tb)
@@ -236,8 +237,10 @@ def tile_mix_lowrank_fm_pl_gelu_kernel(
             if BANKS <= nxt < TILES:
                 for a in range(K_PASSES):
                     base_pass(nxt, a)
-            if j % 2 == 1:
-                store_result(g, j // 2)
+            if g < GROUPS - 1 and j == PACK - 1:
+                store_result(g, slice(0, PACK))
+            if g == GROUPS - 1 and j % 2 == 1:
+                store_result(g, slice(j - 1, j + 1))
             if i == 7:
                 store_words(0)
                 round_plain("vector", res_bf[1], result[1][:], 0)
@@ -248,12 +251,11 @@ def tile_mix_lowrank_fm_pl_gelu_kernel(
             if i == 13:
                 store_words(1)
         store_words(2)
-        round_plain("vector", res_bf[3], result[3][:, :, 0:352], 0)
-        round_plain("scalar", res_bf[3], result[3][:, :, 352:T], 352)
+        round_shared(round_plain, res_bf[3], result[3], VECTOR_SHARE)
         quantise_result(3)
         store_words(3)
         for q4 in range(4):
-            nc.sync.dma_start(
+            nc.scalar.dma_start(
                 out=out_2[:, 4 * q4 : 4 * q4 + 4, :].bitcast(I32),
                 in_=res_scales[32 * q4 : 32 * q4 + 16, :].bitcast(I32),
             )

@@ -64,12 +64,14 @@ def tile_mix_lowrank_fm_pl_gelu_kernel(
             copy(engine, view[:, m0 : m0 + words, :, :], raw.rearrange("p j (m s) -> p m j s", s=PACK))
 
         def round_shared(rounder, dst, raw, split):
-            rounder("scalar", dst, raw[:, :, split:SPAN], split)
-            rounder("vector", dst, raw[:, :, 0:split], 0)
+            if split < SPAN:
+                rounder("scalar", dst, raw[:, :, split:SPAN], split)
+            if split > 0:
+                rounder("vector", dst, raw[:, :, 0:split], 0)
 
         def quantise(codes, scales, grouped):
             nc.vector.quantize_mx(
-                out=codes.bitcast(FP8X4), scales=scales, in_=grouped[:].rearrange("p c j -> p (c j)")
+                out=codes.bitcast(FP8X4), scales=scales, in_=grouped.rearrange("p c j -> p (c j)")
             )
 
         def operand(name):
@@ -84,9 +86,10 @@ def tile_mix_lowrank_fm_pl_gelu_kernel(
         ws_raw = sbuf("ws_raw", [P, K_PASSES, M], U8)
         nc.vector.memset(ws_raw[:].rearrange("p a n -> p (a n)").bitcast(I32), 0)
 
-        def load_w4(a):
-            raw = sbuf("w4_raw%d" % a, [P, 2 * M], U8)
-            nc.sync.dma_start(out=raw[:].bitcast(I32), in_=w4_words[a].bitcast(I32))
+        def load_w4(h):
+            raw = sbuf("w4_raw%d" % h, [P, K_PASSES, M], U8)
+            src = w4_words[:, :, h * M : (h + 1) * M].rearrange("a p c -> p a c")
+            nc.sync.dma_start(out=raw[:].bitcast(I32), in_=src.bitcast(I32))
             return raw
 
         whole = slice(0, SPAN)
@@ -98,30 +101,35 @@ def tile_mix_lowrank_fm_pl_gelu_kernel(
                 in_=w4_scales[:, 4 * q : 4 * q + 4, :].rearrange("a r n -> r a n").bitcast(I32),
             )
         down_raw = [load_rows("down_raw0", down_rows[0], whole)]
-        w4_raw.append(load_w4(1))
         x_raw.append(load_rows("x_raw1", x_rows[1], whole))
         down_raw.append(load_rows("down_raw1", down_rows[1], whole))
+        up_raw = [load_rows("up_raw0", up, whole)]
         bias = sbuf("bias", [P, GROUPS, PACK], F32)
         nc.sync.dma_start(out=bias[:], in_=b.rearrange("(g p j) -> p g j", g=GROUPS, j=PACK))
-        up_raw = [load_rows("up_raw%d" % g, up, slice(g * SPAN, (g + 1) * SPAN)) for g in range(GROUPS)]
+        w4_raw.append(load_w4(1))
+        for g in range(1, GROUPS):
+            up_raw.append(load_rows("up_raw%d" % g, up, slice(g * SPAN, (g + 1) * SPAN)))
 
         xq = [operand("x%d" % a) for a in range(K_PASSES)]
         dq = [operand("down%d" % a) for a in range(K_PASSES)]
         uq = [operand("up%d" % g) for g in range(GROUPS)]
         hq = operand("h")
         ws = sbuf("ws", [P, K_PASSES, M], U8)
-        w4 = [sbuf("w4_%d" % a, [P, 2 * M], U8) for a in range(K_PASSES)]
+        w4 = [sbuf("w4_%d" % h, [P, K_PASSES, M], U8) for h in range(2)]
 
-        def deal_w4(a):
+        def deal_w4(g):
+            h = g // 2
+            cols = slice((g % 2) * 2 * SPAN, (g % 2 + 1) * 2 * SPAN)
             nc.vector.tensor_copy(
-                out=w4[a][:].rearrange("p (g s m e) -> p g s m e", g=GROUPS, s=PACK, e=2),
-                in_=w4_raw[a][:].rearrange("p (g m s e) -> p g s m e", g=GROUPS, s=PACK, e=2),
+                out=w4[h][:, :, cols].rearrange("p a (s m e) -> p a s m e", s=PACK, e=2),
+                in_=w4_raw[h][:, :, cols].rearrange("p a (m s e) -> p a s m e", s=PACK, e=2),
             )
 
-        def deal_ws():
+        def deal_ws(h):
+            cols = slice(h * M // 2, (h + 1) * M // 2)
             nc.vector.tensor_copy(
-                out=ws[:].rearrange("p a (g s m) -> p (a g) s m", g=GROUPS, s=PACK),
-                in_=ws_raw[:].rearrange("p a (g m s) -> p (a g) s m", g=GROUPS, s=PACK),
+                out=ws[:, :, cols].rearrange("p a (g s m) -> p a g s m", g=2, s=PACK),
+                in_=ws_raw[:, :, cols].rearrange("p a (g m s) -> p a g s m", g=2, s=PACK),
             )
 
         def bank(i, shape):
@@ -150,7 +158,7 @@ def tile_mix_lowrank_fm_pl_gelu_kernel(
                 y_ps[i] = bank(i, [P, T])
             nc.tensor.matmul_mx(
                 out=y_ps[i][:],
-                lhsT=w4[a][:, 2 * P * i : 2 * P * (i + 1)].bitcast(FP4X4),
+                lhsT=w4[i // BANKS][:, a, 2 * P * (i % BANKS) : 2 * P * (i % BANKS + 1)].bitcast(FP4X4),
                 lhsT_scale=ws[:, a, P * i : P * (i + 1)],
                 rhs=xq[a][1][:].bitcast(FP8X4),
                 rhs_scale=xq[a][2][:],
@@ -181,8 +189,8 @@ def tile_mix_lowrank_fm_pl_gelu_kernel(
             rows = out_0[g * SPAN : (g + 1) * SPAN, :].rearrange("(p j) t -> p j t", j=PACK)
             nc.sync.dma_start(out=rows[:, slots, :], in_=result[g][:, slots, :])
 
-        def quantise_result(g):
-            quantise(res_codes[g][:], res_scales[PACK * g : P, :], res_bf[g])
+        def quantise_result(g, cols=slice(0, T)):
+            quantise(res_codes[g][:, cols], res_scales[PACK * g : P, cols], res_bf[g][:, cols, :])
 
         def store_words(g):
             nc.sync.dma_start(
@@ -190,68 +198,72 @@ def tile_mix_lowrank_fm_pl_gelu_kernel(
             )
 
         def q(op):
-            quantise(op[1][:], op[2][:], op[0])
+            quantise(op[1][:], op[2][:], op[0][:])
 
         deal_w4(0)
-        round_shared(round_plain, xq[0][0], x_raw[0], VECTOR_SHARE)
-        q(xq[0])
-        deal_ws()
-        round_dealt("scalar", dq[0][0], down_raw[0][:], 0)
         deal_w4(1)
+        round_shared(round_plain, xq[0][0], x_raw[0], 352)
+        deal_ws(0)
+        q(xq[0])
+        for i in range(PACK):
+            base_pass(i, 0)
+        round_shared(round_dealt, dq[0][0], down_raw[0], 192)
+        deal_ws(1)
         q(dq[0])
         for tb in range(PACK):
             h_pass(0, tb)
-        for i in range(PACK):
-            base_pass(i, 0)
-        round_shared(round_plain, xq[1][0], x_raw[1], HALF)
+        round_shared(round_plain, xq[1][0], x_raw[1], 288)
         q(xq[1])
         for i in range(PACK):
             base_pass(i, 1)
-        round_shared(round_dealt, dq[1][0], down_raw[1], VECTOR_SHARE)
+        round_shared(round_dealt, dq[1][0], down_raw[1], 352)
         q(dq[1])
+        round_shared(round_dealt, uq[0][0], up_raw[0], 512)
+        q(uq[0])
         for tb in range(PACK):
             h_pass(1, tb)
             nc.scalar.copy(out=hq[0][:, tb * P : (tb + 1) * P, :], in_=h_ps[tb][:].rearrange("p j t -> p t j"))
-        round_dealt("vector", uq[0][0], up_raw[0][:], 0)
-        q(uq[0])
-        q(hq)
+        deal_w4(2)
+        for cols in (slice(0, 256), slice(256, T)):
+            quantise(hq[1][:, cols], hq[2][:, cols], hq[0][:, cols, :])
         for i in range(PACK, BANKS):
             for a in range(K_PASSES):
                 base_pass(i, a)
+        round_shared(round_dealt, uq[1][0], up_raw[1], 256)
+        deal_w4(3)
+        q(uq[1])
 
-        lag = 2
+        late = [(i, a) for i in range(BANKS, TILES) for a in range(K_PASSES)]
+        first, last = 2, 14
+        done = 0
         for i in range(TILES):
             g, j = divmod(i, PACK)
-            if j == 0 and g == 0:
-                round_dealt("vector", uq[1][0], up_raw[1][:], 0)
-                q(uq[1])
-                round_dealt("vector", uq[2][0], up_raw[2][:], 0)
-                q(uq[2])
-                round_dealt("vector", uq[3][0], up_raw[3][:], 0)
-            if i == PACK:
-                round_plain("vector", res_bf[0], result[0][:], 0)
-                q(uq[3])
-                quantise_result(0)
             finish_tile(i)
-            nxt = i + BANKS - lag
-            if BANKS <= nxt < TILES:
-                for a in range(K_PASSES):
-                    base_pass(nxt, a)
-            if g < GROUPS - 1 and j == PACK - 1:
-                store_result(g, slice(0, PACK))
-            if g == GROUPS - 1 and j % 2 == 1:
+            want = min(len(late), max(0, -(-(i - first + 1) * len(late) // (last - first + 1))))
+            while done < want:
+                base_pass(*late[done])
+                done = done + 1
+            if j % 2 == 1:
                 store_result(g, slice(j - 1, j + 1))
+            if i == 3:
+                round_shared(round_dealt, uq[2][0], up_raw[2], SPAN)
+                round_plain("vector", res_bf[0], result[0][:], 0)
+                q(uq[2])
+                round_shared(round_dealt, uq[3][0], up_raw[3], SPAN)
+                quantise_result(0)
+                q(uq[3])
             if i == 7:
-                store_words(0)
                 round_plain("vector", res_bf[1], result[1][:], 0)
+                quantise_result(1)
             if i == 11:
                 round_plain("vector", res_bf[2], result[2][:], 0)
-                quantise_result(1)
                 quantise_result(2)
-            if i == 13:
+            if i == 9:
+                store_words(0)
+            if i == 11:
                 store_words(1)
         store_words(2)
-        round_shared(round_plain, res_bf[3], result[3], VECTOR_SHARE)
+        round_shared(round_plain, res_bf[3], result[3], 352)
         quantise_result(3)
         store_words(3)
         for q4 in range(4):

@@ -17,12 +17,17 @@ GELU = mybir.ActivationFunctionType.Gelu_apprx_tanh
 P = 128
 PACK = 4
 SPAN = P * PACK
+QUADRANT = 32
+FP4_BYTES = 2
 K_PASSES = K // SPAN
 GROUPS = M // SPAN
 TILES = M // P
 BANKS = 8
-HALF = SPAN // 2
-VECTOR_SHARE = 352
+
+VECTOR_COLS_X0 = 128
+VECTOR_COLS_DOWN1 = 192
+VECTOR_COLS_LAST = 256
+EARLY_TILES = 6
 
 
 def tile_mix_lowrank_fm_pl_gelu_kernel(
@@ -30,244 +35,235 @@ def tile_mix_lowrank_fm_pl_gelu_kernel(
 ):
     nc = tc.nc
     with ExitStack() as ctx:
-        sb = ctx.enter_context(tc.tile_pool(name="sb", bufs=1))
-        ps = ctx.enter_context(tc.psum_pool(name="ps", bufs=1))
+        sbuf_pool = ctx.enter_context(tc.tile_pool(name="sbuf", bufs=1))
+        psum_pool = ctx.enter_context(tc.psum_pool(name="psum", bufs=1))
         ctx.enter_context(tc.manual_schedule())
 
         def sbuf(name, shape, dtype):
-            return sb.tile(shape, dtype, name=name, align_bytes=64)
+            return sbuf_pool.tile(shape, dtype, name=name, align_bytes=64)
 
-        def load_rows(name, src, cols):
-            width = cols.stop - cols.start
-            raw = sbuf(name, [P, PACK, width], F32)
-            nc.sync.dma_start(out=raw[:], in_=src[:, cols].rearrange("(p j) c -> p j c", j=PACK))
+        def bank(number, shape):
+            return psum_pool.tile(shape, F32, name="bank%d" % (number % BANKS))
+
+        def span(number):
+            return slice(number * SPAN, (number + 1) * SPAN)
+
+        def block(number):
+            return slice(number * P, (number + 1) * P)
+
+        w4_scales_raw = sbuf("w4_scales_raw", [P, K_PASSES, M], U8)
+        nc.vector.memset(w4_scales_raw[:].rearrange("p a n -> p (a n)").bitcast(I32), 0)
+        warm = sbuf("warm", [P, 2], F32)
+        nc.vector.memset(warm[:, 0:1], 0.0)
+        nc.scalar.activation(out=warm[:, 1:2], in_=warm[:, 0:1], func=GELU)
+
+        def load_rows(name, rows):
+            raw = sbuf(name, [P, PACK, SPAN], F32)
+            nc.sync.dma_start(out=raw[:], in_=rows.rearrange("(p j) c -> p j c", j=PACK))
             return raw
 
-        def copy(engine, out, in_):
-            if engine == "scalar":
-                nc.scalar.copy(out=out, in_=in_)
-            else:
-                nc.vector.tensor_copy(out=out, in_=in_)
+        def load_w4_words(a):
+            raw = sbuf("w4_words_raw%d" % a, [P, FP4_BYTES * M], U8)
+            nc.sync.dma_start(out=raw[:].bitcast(I32), in_=w4_words[a].bitcast(I32))
+            return raw
 
-        def round_plain(engine, dst, raw, first):
-            width = raw.shape[2]
-            copy(
-                engine,
-                dst[:, first : first + width, :].rearrange("p (c i) j -> p c j i", i=PACK),
-                raw.rearrange("p j (c i) -> p c j i", i=PACK),
+        w4_words_raw = [load_w4_words(0)]
+        x_raw = [load_rows("x_raw0", x[span(0), :])]
+        for r in range(PACK):
+            nc.sync.dma_start(
+                out=w4_scales_raw[r:P:QUADRANT, :, :].bitcast(I32),
+                in_=w4_scales.rearrange("a (q r) n -> r q a n", r=PACK)[r].bitcast(I32),
             )
-
-        def round_dealt(engine, dst, raw, first):
-            words = raw.shape[2] // PACK
-            m0 = first // PACK
-            view = dst[:].rearrange("p (s m) j -> p m j s", s=PACK)
-            copy(engine, view[:, m0 : m0 + words, :, :], raw.rearrange("p j (m s) -> p m j s", s=PACK))
-
-        def round_shared(rounder, dst, raw, split):
-            if split < SPAN:
-                rounder("scalar", dst, raw[:, :, split:SPAN], split)
-            if split > 0:
-                rounder("vector", dst, raw[:, :, 0:split], 0)
-
-        def quantise(codes, scales, grouped):
-            nc.vector.quantize_mx(
-                out=codes.bitcast(FP8X4), scales=scales, in_=grouped.rearrange("p c j -> p (c j)")
-            )
+        down_raw = [load_rows("down_raw0", down[span(0), :])]
+        w4_words_raw.append(load_w4_words(1))
+        down_raw.append(load_rows("down_raw1", down[span(1), :]))
+        x_raw.append(load_rows("x_raw1", x[span(1), :]))
+        up_raw = [load_rows("up_raw0", up[:, span(0)])]
+        bias = sbuf("bias", [P, GROUPS, 2 * PACK], F32)
+        nc.sync.dma_start(out=bias[:, :, 0:PACK], in_=b.rearrange("(g p s) -> p g s", g=GROUPS, s=PACK))
+        for g in range(1, GROUPS):
+            up_raw.append(load_rows("up_raw%d" % g, up[:, span(g)]))
 
         def operand(name):
-            grouped = sbuf(name + "_bf", [P, SPAN, PACK], BF16)
-            codes = sbuf(name + "_codes", [P, SPAN], U32)
+            rounded = sbuf(name + "_rounded", [P, SPAN, PACK], BF16)
+            words = sbuf(name + "_words", [P, SPAN], U32)
             scales = sbuf(name + "_scales", [P, SPAN], U8)
-            return grouped, codes, scales
+            return rounded, words, scales
 
-        x_rows = [x[a * SPAN : (a + 1) * SPAN, :] for a in range(K_PASSES)]
-        down_rows = [down[a * SPAN : (a + 1) * SPAN, :] for a in range(K_PASSES)]
+        x_mx = [operand("x%d" % a) for a in range(K_PASSES)]
+        down_mx = [operand("down%d" % a) for a in range(K_PASSES)]
+        up_mx = [operand("up%d" % g) for g in range(GROUPS)]
+        h_mx = operand("h")
 
-        ws_raw = sbuf("ws_raw", [P, K_PASSES, M], U8)
-        nc.vector.memset(ws_raw[:].rearrange("p a n -> p (a n)").bitcast(I32), 0)
-
-        def load_w4(h):
-            raw = sbuf("w4_raw%d" % h, [P, K_PASSES, M], U8)
-            src = w4_words[:, :, h * M : (h + 1) * M].rearrange("a p c -> p a c")
-            nc.sync.dma_start(out=raw[:].bitcast(I32), in_=src.bitcast(I32))
-            return raw
-
-        whole = slice(0, SPAN)
-        w4_raw = [load_w4(0)]
-        x_raw = [load_rows("x_raw0", x_rows[0], whole)]
-        for q in range(4):
-            nc.sync.dma_start(
-                out=ws_raw[32 * q : 32 * q + 4, :, :].bitcast(I32),
-                in_=w4_scales[:, 4 * q : 4 * q + 4, :].rearrange("a r n -> r a n").bitcast(I32),
+        def round_plain(copy, rounded, raw, cols):
+            copy(
+                out=rounded[:, cols, :].rearrange("p (c i) j -> p c j i", i=PACK),
+                in_=raw[:, :, cols].rearrange("p j (c i) -> p c j i", i=PACK),
             )
-        down_raw = [load_rows("down_raw0", down_rows[0], whole)]
-        x_raw.append(load_rows("x_raw1", x_rows[1], whole))
-        down_raw.append(load_rows("down_raw1", down_rows[1], whole))
-        up_raw = [load_rows("up_raw0", up, whole)]
-        bias = sbuf("bias", [P, GROUPS, PACK], F32)
-        nc.sync.dma_start(out=bias[:], in_=b.rearrange("(g p j) -> p g j", g=GROUPS, j=PACK))
-        w4_raw.append(load_w4(1))
-        for g in range(1, GROUPS):
-            up_raw.append(load_rows("up_raw%d" % g, up, slice(g * SPAN, (g + 1) * SPAN)))
 
-        xq = [operand("x%d" % a) for a in range(K_PASSES)]
-        dq = [operand("down%d" % a) for a in range(K_PASSES)]
-        uq = [operand("up%d" % g) for g in range(GROUPS)]
-        hq = operand("h")
-        ws = sbuf("ws", [P, K_PASSES, M], U8)
-        w4 = [sbuf("w4_%d" % h, [P, K_PASSES, M], U8) for h in range(2)]
+        def round_dealt(copy, rounded, raw, cols):
+            dealt = rounded[:].rearrange("p (s m) j -> p m j s", s=PACK)
+            copy(
+                out=dealt[:, cols.start // PACK : cols.stop // PACK, :, :],
+                in_=raw[:, :, cols].rearrange("p j (m s) -> p m j s", s=PACK),
+            )
 
-        def deal_w4(g):
-            h = g // 2
-            cols = slice((g % 2) * 2 * SPAN, (g % 2 + 1) * 2 * SPAN)
+        def round_shared(rounder, rounded, raw, vector_cols):
+            rounder(nc.scalar.copy, rounded, raw, slice(vector_cols, SPAN))
+            rounder(nc.vector.tensor_copy, rounded, raw, slice(0, vector_cols))
+
+        def quantise(mx, cols=span(0)):
+            rounded, words, scales = mx
+            nc.vector.quantize_mx(
+                out=words[:, cols].bitcast(FP8X4),
+                scales=scales[:, cols],
+                in_=rounded[:, cols, :].rearrange("p c j -> p (c j)"),
+            )
+
+        w4_words_dealt = [sbuf("w4_words_dealt%d" % a, [P, FP4_BYTES * M], U8) for a in range(K_PASSES)]
+        w4_scales_dealt = [sbuf("w4_scales_dealt%d" % a, [P, M], U8) for a in range(K_PASSES)]
+
+        def deal_w4_words(a):
             nc.vector.tensor_copy(
-                out=w4[h][:, :, cols].rearrange("p a (s m e) -> p a s m e", s=PACK, e=2),
-                in_=w4_raw[h][:, :, cols].rearrange("p a (m s e) -> p a s m e", s=PACK, e=2),
+                out=w4_words_dealt[a][:].rearrange("p (g s m e) -> p g s m e", g=GROUPS, s=PACK, e=FP4_BYTES),
+                in_=w4_words_raw[a][:].rearrange("p (g m s e) -> p g s m e", g=GROUPS, s=PACK, e=FP4_BYTES),
             )
 
-        def deal_ws(h):
-            cols = slice(h * M // 2, (h + 1) * M // 2)
+        def deal_w4_scales(a):
             nc.vector.tensor_copy(
-                out=ws[:, :, cols].rearrange("p a (g s m) -> p a g s m", g=2, s=PACK),
-                in_=ws_raw[:, :, cols].rearrange("p a (g m s) -> p a g s m", g=2, s=PACK),
+                out=w4_scales_dealt[a][:].rearrange("p (g s m) -> p g s m", g=GROUPS, s=PACK),
+                in_=w4_scales_raw[:, a, :].rearrange("p (g m s) -> p g s m", g=GROUPS, s=PACK),
             )
 
-        def bank(i, shape):
-            return ps.tile(shape, F32, name="bank%d" % (i % BANKS))
+        h_psum = [bank(PACK + tb, [P, PACK, P]) for tb in range(PACK)]
 
-        h_ps = [bank(GROUPS + tb, [P, PACK, P]) for tb in range(PACK)]
-
-        def h_pass(a, tb):
-            t_cols = slice(tb * P, (tb + 1) * P)
-            for j in range(PACK):
-                r_cols = slice(j * P, (j + 1) * P)
+        def h_passes(a, tb):
+            for s in range(PACK):
                 nc.tensor.matmul_mx(
-                    out=h_ps[tb][:, j, :],
-                    lhsT=dq[a][1][:, r_cols].bitcast(FP8X4),
-                    lhsT_scale=dq[a][2][:, r_cols],
-                    rhs=xq[a][1][:, t_cols].bitcast(FP8X4),
-                    rhs_scale=xq[a][2][:, t_cols],
-                    start=(a == 0 and j == 0),
-                    stop=(a == K_PASSES - 1 and j == PACK - 1),
+                    out=h_psum[tb][:, s, :],
+                    lhsT=down_mx[a][1][:, block(s)].bitcast(FP8X4),
+                    lhsT_scale=down_mx[a][2][:, block(s)],
+                    rhs=x_mx[a][1][:, block(tb)].bitcast(FP8X4),
+                    rhs_scale=x_mx[a][2][:, block(tb)],
+                    start=(a == 0 and s == 0),
+                    stop=(a == K_PASSES - 1 and s == PACK - 1),
                 )
 
-        y_ps = {}
+        y_psum = {}
 
-        def base_pass(i, a):
+        def w4_pass(i, a):
             if a == 0:
-                y_ps[i] = bank(i, [P, T])
+                y_psum[i] = bank(i, [P, T])
             nc.tensor.matmul_mx(
-                out=y_ps[i][:],
-                lhsT=w4[i // BANKS][:, a, 2 * P * (i % BANKS) : 2 * P * (i % BANKS + 1)].bitcast(FP4X4),
-                lhsT_scale=ws[:, a, P * i : P * (i + 1)],
-                rhs=xq[a][1][:].bitcast(FP8X4),
-                rhs_scale=xq[a][2][:],
+                out=y_psum[i][:],
+                lhsT=w4_words_dealt[a][:, FP4_BYTES * P * i : FP4_BYTES * P * (i + 1)].bitcast(FP4X4),
+                lhsT_scale=w4_scales_dealt[a][:, block(i)],
+                rhs=x_mx[a][1][:].bitcast(FP8X4),
+                rhs_scale=x_mx[a][2][:],
                 start=(a == 0),
                 stop=False,
             )
 
         result = [sbuf("result%d" % g, [P, PACK, T], F32) for g in range(GROUPS)]
-        res_bf = [sbuf("res_bf%d" % g, [P, T, PACK], BF16) for g in range(GROUPS)]
-        res_codes = [sbuf("res_codes%d" % g, [P, T], U32) for g in range(GROUPS)]
-        res_scales = sbuf("res_scales", [P, T], U8)
+        result_scales = sbuf("result_scales", [P, T], U8)
+        result_mx = [
+            (
+                sbuf("result_rounded%d" % g, [P, T, PACK], BF16),
+                sbuf("result_words%d" % g, [P, T], U32),
+                result_scales[PACK * g : P, :],
+            )
+            for g in range(GROUPS)
+        ]
 
         def finish_tile(i):
-            g, j = divmod(i, PACK)
-            cols = slice(j * P, (j + 1) * P)
+            g, s = divmod(i, PACK)
             nc.tensor.matmul_mx(
-                out=y_ps[i][:],
-                lhsT=uq[g][1][:, cols].bitcast(FP8X4),
-                lhsT_scale=uq[g][2][:, cols],
-                rhs=hq[1][:].bitcast(FP8X4),
-                rhs_scale=hq[2][:],
+                out=y_psum[i][:],
+                lhsT=up_mx[g][1][:, block(s)].bitcast(FP8X4),
+                lhsT_scale=up_mx[g][2][:, block(s)],
+                rhs=h_mx[1][:].bitcast(FP8X4),
+                rhs_scale=h_mx[2][:],
                 start=False,
                 stop=True,
             )
-            nc.scalar.activation(out=result[g][:, j, :], in_=y_ps[i][:], func=GELU, bias=bias[:, g, j : j + 1])
+            nc.scalar.activation(out=result[g][:, s, :], in_=y_psum[i][:], func=GELU, bias=bias[:, g, s : s + 1])
 
-        def store_result(g, slots):
-            rows = out_0[g * SPAN : (g + 1) * SPAN, :].rearrange("(p j) t -> p j t", j=PACK)
-            nc.sync.dma_start(out=rows[:, slots, :], in_=result[g][:, slots, :])
-
-        def quantise_result(g, cols=slice(0, T)):
-            quantise(res_codes[g][:, cols], res_scales[PACK * g : P, cols], res_bf[g][:, cols, :])
+        def store_pair(g, s):
+            rows = out_0[span(g), :].rearrange("(p s) t -> p s t", s=PACK)
+            nc.sync.dma_start(out=rows[:, s : s + 2, :], in_=result[g][:, s : s + 2, :])
 
         def store_words(g):
             nc.sync.dma_start(
-                out=out_1[g].rearrange("p t i -> p (t i)").bitcast(I32), in_=res_codes[g][:].bitcast(I32)
+                out=out_1[g].rearrange("p t i -> p (t i)").bitcast(I32), in_=result_mx[g][1][:].bitcast(I32)
             )
 
-        def q(op):
-            quantise(op[1][:], op[2][:], op[0][:])
+        def round_on_vector(rounder, mx, raw):
+            rounder(nc.vector.tensor_copy, mx[0], raw, span(0))
 
-        deal_w4(0)
-        deal_w4(1)
-        round_shared(round_plain, xq[0][0], x_raw[0], 352)
-        deal_ws(0)
-        q(xq[0])
-        for i in range(PACK):
-            base_pass(i, 0)
-        round_shared(round_dealt, dq[0][0], down_raw[0], 192)
-        deal_ws(1)
-        q(dq[0])
+        deal_w4_words(0)
+        round_shared(round_plain, x_mx[0][0], x_raw[0], VECTOR_COLS_X0)
+        deal_w4_scales(0)
+        quantise(x_mx[0])
+        for i in range(BANKS - PACK):
+            w4_pass(i, 0)
+        round_dealt(nc.scalar.copy, down_mx[0][0], down_raw[0], span(0))
+        deal_w4_scales(1)
+        deal_w4_words(1)
+        quantise(down_mx[0])
         for tb in range(PACK):
-            h_pass(0, tb)
-        round_shared(round_plain, xq[1][0], x_raw[1], 288)
-        q(xq[1])
-        for i in range(PACK):
-            base_pass(i, 1)
-        round_shared(round_dealt, dq[1][0], down_raw[1], 352)
-        q(dq[1])
-        round_shared(round_dealt, uq[0][0], up_raw[0], 512)
-        q(uq[0])
+            h_passes(0, tb)
+
+        round_shared(round_dealt, down_mx[1][0], down_raw[1], VECTOR_COLS_DOWN1)
+        quantise(down_mx[1])
+        round_plain(nc.scalar.copy, x_mx[1][0], x_raw[1], block(PACK - 1))
+        round_plain(nc.vector.tensor_copy, x_mx[1][0], x_raw[1], block(0))
         for tb in range(PACK):
-            h_pass(1, tb)
-            nc.scalar.copy(out=hq[0][:, tb * P : (tb + 1) * P, :], in_=h_ps[tb][:].rearrange("p j t -> p t j"))
-        deal_w4(2)
-        for cols in (slice(0, 256), slice(256, T)):
-            quantise(hq[1][:, cols], hq[2][:, cols], hq[0][:, cols, :])
-        for i in range(PACK, BANKS):
+            if tb + 1 < PACK - 1:
+                round_plain(nc.vector.tensor_copy, x_mx[1][0], x_raw[1], block(tb + 1))
+            quantise(x_mx[1], block(tb))
+            h_passes(1, tb)
+            nc.scalar.copy(out=h_mx[0][:, block(tb), :], in_=h_psum[tb][:].rearrange("p s t -> p t s"))
+        for i in range(BANKS - PACK):
+            w4_pass(i, 1)
+        round_on_vector(round_dealt, up_mx[0], up_raw[0])
+        quantise(h_mx, slice(0, T // 2))
+        quantise(up_mx[0])
+        quantise(h_mx, slice(T // 2, T))
+        for i in range(BANKS - PACK, EARLY_TILES):
             for a in range(K_PASSES):
-                base_pass(i, a)
-        round_shared(round_dealt, uq[1][0], up_raw[1], 256)
-        deal_w4(3)
-        q(uq[1])
+                w4_pass(i, a)
+        round_on_vector(round_dealt, up_mx[1], up_raw[1])
+        quantise(up_mx[1])
 
-        late = [(i, a) for i in range(BANKS, TILES) for a in range(K_PASSES)]
-        first, last = 2, 14
-        done = 0
+        late_passes = [(i, a) for i in range(EARLY_TILES, TILES) for a in range(K_PASSES)]
+        issued = 0
         for i in range(TILES):
-            g, j = divmod(i, PACK)
+            g, s = divmod(i, PACK)
             finish_tile(i)
-            want = min(len(late), max(0, -(-(i - first + 1) * len(late) // (last - first + 1))))
-            while done < want:
-                base_pass(*late[done])
-                done = done + 1
-            if j % 2 == 1:
-                store_result(g, slice(j - 1, j + 1))
-            if i == 3:
-                round_shared(round_dealt, uq[2][0], up_raw[2], SPAN)
-                round_plain("vector", res_bf[0], result[0][:], 0)
-                q(uq[2])
-                round_shared(round_dealt, uq[3][0], up_raw[3], SPAN)
-                quantise_result(0)
-                q(uq[3])
-            if i == 7:
-                round_plain("vector", res_bf[1], result[1][:], 0)
-                quantise_result(1)
-            if i == 11:
-                round_plain("vector", res_bf[2], result[2][:], 0)
-                quantise_result(2)
-            if i == 9:
-                store_words(0)
-            if i == 11:
-                store_words(1)
-        store_words(2)
-        round_shared(round_plain, res_bf[3], result[3], 352)
-        quantise_result(3)
-        store_words(3)
-        for q4 in range(4):
+            due = min(len(late_passes), -(-(i + 1) * len(late_passes) // (TILES - 1)))
+            for late in late_passes[issued:due]:
+                w4_pass(*late)
+            issued = due
+            if s % 2 == 1:
+                store_pair(g, s - 1)
+            if s == 1 and g >= 2:
+                store_words(g - 2)
+            if s == PACK - 1 and g == 0:
+                round_on_vector(round_dealt, up_mx[2], up_raw[2])
+                quantise(up_mx[2])
+                round_on_vector(round_plain, result_mx[0], result[0])
+                round_on_vector(round_dealt, up_mx[3], up_raw[3])
+                quantise(result_mx[0])
+                quantise(up_mx[3])
+            if s == PACK - 1 and 0 < g < GROUPS - 1:
+                round_on_vector(round_plain, result_mx[g], result[g])
+                quantise(result_mx[g])
+        store_words(GROUPS - 2)
+        round_shared(round_plain, result_mx[GROUPS - 1][0], result[GROUPS - 1], VECTOR_COLS_LAST)
+        quantise(result_mx[GROUPS - 1])
+        store_words(GROUPS - 1)
+        for q in range(P // QUADRANT):
             nc.scalar.dma_start(
-                out=out_2[:, 4 * q4 : 4 * q4 + 4, :].bitcast(I32),
-                in_=res_scales[32 * q4 : 32 * q4 + 16, :].bitcast(I32),
+                out=out_2[:, PACK * q : PACK * (q + 1), :].bitcast(I32),
+                in_=result_scales[QUADRANT * q : QUADRANT * q + GROUPS * PACK, :].bitcast(I32),
             )

@@ -1,6 +1,7 @@
 from contextlib import ExitStack
 
 import concourse.mybir as mybir
+from concourse.masks import make_identity
 
 K, R, M, T = 1024, 512, 2048, 512
 FLOPS = 2 * T * (K * R + K * M + R * M)
@@ -22,11 +23,12 @@ FP4_BYTES = 2
 K_PASSES = K // SPAN
 GROUPS = M // SPAN
 TILES = M // P
+BIAS_ROW = 8
 BANKS = 8
 
 VECTOR_COLS_X0 = 128
 VECTOR_COLS_DOWN1 = 192
-VECTOR_COLS_LAST = 256
+VECTOR_COLS_LAST = 208
 EARLY_TILES = 6
 
 
@@ -53,6 +55,10 @@ def tile_mix_lowrank_fm_pl_gelu_kernel(
 
         w4_scales_raw = sbuf("w4_scales_raw", [P, K_PASSES, M], U8)
         nc.vector.memset(w4_scales_raw[:].rearrange("p a n -> p (a n)").bitcast(I32), 0)
+        bias_rows = sbuf("bias_rows", [P, SPAN], F32)
+        nc.vector.memset(bias_rows[:], 0.0)
+        identity = sbuf("identity", [P, P], F32)
+        make_identity(nc, identity[:])
         warm = sbuf("warm", [P, 2], F32)
         nc.vector.memset(warm[:, 0:1], 0.0)
         nc.scalar.activation(out=warm[:, 1:2], in_=warm[:, 0:1], func=GELU)
@@ -74,15 +80,12 @@ def tile_mix_lowrank_fm_pl_gelu_kernel(
                 out=w4_scales_raw[r:P:QUADRANT, :, :].bitcast(I32),
                 in_=w4_scales.rearrange("a (q r) n -> r q a n", r=PACK)[r].bitcast(I32),
             )
+        nc.sync.dma_start(out=bias_rows[BIAS_ROW:P:QUADRANT, :], in_=b.rearrange("(g c) -> g c", g=GROUPS))
         down_raw = [load_rows("down_raw0", down[span(0), :])]
         w4_words_raw.append(load_w4_words(1))
         down_raw.append(load_rows("down_raw1", down[span(1), :]))
         x_raw.append(load_rows("x_raw1", x[span(1), :]))
-        up_raw = [load_rows("up_raw0", up[:, span(0)])]
-        bias = sbuf("bias", [P, GROUPS, 2 * PACK], F32)
-        nc.sync.dma_start(out=bias[:, :, 0:PACK], in_=b.rearrange("(g p s) -> p g s", g=GROUPS, s=PACK))
-        for g in range(1, GROUPS):
-            up_raw.append(load_rows("up_raw%d" % g, up[:, span(g)]))
+        up_raw = [load_rows("up_raw%d" % g, up[:, span(g)]) for g in range(GROUPS)]
 
         def operand(name):
             rounded = sbuf(name + "_rounded", [P, SPAN, PACK], BF16)
@@ -186,7 +189,7 @@ def tile_mix_lowrank_fm_pl_gelu_kernel(
                 start=False,
                 stop=True,
             )
-            nc.scalar.activation(out=result[g][:, s, :], in_=y_psum[i][:], func=GELU, bias=bias[:, g, s : s + 1])
+            nc.scalar.activation(out=result[g][:, s, :], in_=y_psum[i][:], func=GELU, bias=bias[:, s, g : g + 1])
 
         def store_pair(g, s):
             rows = out_0[span(g), :].rearrange("(p s) t -> p s t", s=PACK)
@@ -202,6 +205,11 @@ def tile_mix_lowrank_fm_pl_gelu_kernel(
 
         deal_w4_words(0)
         round_shared(round_plain, x_mx[0][0], x_raw[0], VECTOR_COLS_X0)
+        bias_psum = bank(0, [P, PACK, P])
+        for s in range(PACK):
+            nc.tensor.transpose(bias_psum[:, s, :], bias_rows[:, s:SPAN:PACK], identity[:])
+        bias = sbuf("bias", [P, PACK, GROUPS], F32)
+        nc.scalar.copy(out=bias[:], in_=bias_psum[:, :, BIAS_ROW:P:QUADRANT])
         deal_w4_scales(0)
         quantise(x_mx[0])
         for i in range(BANKS - PACK):
@@ -240,25 +248,27 @@ def tile_mix_lowrank_fm_pl_gelu_kernel(
         for i in range(TILES):
             g, s = divmod(i, PACK)
             finish_tile(i)
-            due = min(len(late_passes), -(-(i + 1) * len(late_passes) // (TILES - 1)))
+            due = min(len(late_passes), (i + 1) * len(late_passes) // (TILES - 1))
             for late in late_passes[issued:due]:
                 w4_pass(*late)
             issued = due
             if s % 2 == 1:
                 store_pair(g, s - 1)
-            if s == 1 and g >= 2:
-                store_words(g - 2)
             if s == PACK - 1 and g == 0:
                 round_on_vector(round_dealt, up_mx[2], up_raw[2])
                 quantise(up_mx[2])
                 round_on_vector(round_plain, result_mx[0], result[0])
                 round_on_vector(round_dealt, up_mx[3], up_raw[3])
-                quantise(result_mx[0])
                 quantise(up_mx[3])
-            if s == PACK - 1 and 0 < g < GROUPS - 1:
-                round_on_vector(round_plain, result_mx[g], result[g])
-                quantise(result_mx[g])
-        store_words(GROUPS - 2)
+                quantise(result_mx[0])
+            if s == PACK - 1 and g == GROUPS - 2:
+                store_words(0)
+                for middle in range(1, GROUPS - 1):
+                    round_on_vector(round_plain, result_mx[middle], result[middle])
+                for middle in range(1, GROUPS - 1):
+                    quantise(result_mx[middle])
+        for middle in range(1, GROUPS - 1):
+            store_words(middle)
         round_shared(round_plain, result_mx[GROUPS - 1][0], result[GROUPS - 1], VECTOR_COLS_LAST)
         quantise(result_mx[GROUPS - 1])
         store_words(GROUPS - 1)

@@ -10,6 +10,7 @@ F32 = mybir.dt.float32
 BF16 = mybir.dt.bfloat16
 I32 = mybir.dt.int32
 U32 = mybir.dt.uint32
+U16 = mybir.dt.uint16
 U8 = mybir.dt.uint8
 FP8X4 = mybir.dt.float8_e4m3fn_x4
 FP4X4 = mybir.dt.float4_e2m1fn_x4
@@ -26,9 +27,7 @@ TILES = M // P
 BIAS_ROW = 8
 BANKS = 8
 
-VECTOR_COLS_X0 = 128
-VECTOR_COLS_DOWN1 = 192
-VECTOR_COLS_LAST = 208
+VECTOR_COLS_LAST = 288
 EARLY_TILES = 6
 
 
@@ -47,11 +46,14 @@ def tile_mix_lowrank_fm_pl_gelu_kernel(
         def bank(number, shape):
             return psum_pool.tile(shape, F32, name="bank%d" % (number % BANKS))
 
+        def part(number, width):
+            return slice(number * width, (number + 1) * width)
+
         def span(number):
-            return slice(number * SPAN, (number + 1) * SPAN)
+            return part(number, SPAN)
 
         def block(number):
-            return slice(number * P, (number + 1) * P)
+            return part(number, P)
 
         w4_scales_raw = sbuf("w4_scales_raw", [P, K_PASSES, M], U8)
         nc.vector.memset(w4_scales_raw[:].rearrange("p a n -> p (a n)").bitcast(I32), 0)
@@ -59,21 +61,12 @@ def tile_mix_lowrank_fm_pl_gelu_kernel(
         nc.vector.memset(bias_rows[:], 0.0)
         identity = sbuf("identity", [P, P], F32)
         make_identity(nc, identity[:])
-        warm = sbuf("warm", [P, 2], F32)
-        nc.vector.memset(warm[:, 0:1], 0.0)
-        nc.scalar.activation(out=warm[:, 1:2], in_=warm[:, 0:1], func=GELU)
 
         def load_rows(name, rows):
-            raw = sbuf(name, [P, PACK, SPAN], F32)
+            raw = sbuf(name, [P, PACK, rows.shape[1]], F32)
             nc.sync.dma_start(out=raw[:], in_=rows.rearrange("(p j) c -> p j c", j=PACK))
             return raw
 
-        def load_w4_words(a):
-            raw = sbuf("w4_words_raw%d" % a, [P, FP4_BYTES * M], U8)
-            nc.sync.dma_start(out=raw[:].bitcast(I32), in_=w4_words[a].bitcast(I32))
-            return raw
-
-        w4_words_raw = [load_w4_words(0)]
         x_raw = [load_rows("x_raw0", x[span(0), :])]
         for r in range(PACK):
             nc.sync.dma_start(
@@ -81,11 +74,13 @@ def tile_mix_lowrank_fm_pl_gelu_kernel(
                 in_=w4_scales.rearrange("a (q r) n -> r q a n", r=PACK)[r].bitcast(I32),
             )
         nc.sync.dma_start(out=bias_rows[BIAS_ROW:P:QUADRANT, :], in_=b.rearrange("(g c) -> g c", g=GROUPS))
-        down_raw = [load_rows("down_raw0", down[span(0), :])]
-        w4_words_raw.append(load_w4_words(1))
-        down_raw.append(load_rows("down_raw1", down[span(1), :]))
+        down_raw = [load_rows("down_raw%d" % a, down[span(a), :]) for a in range(K_PASSES)]
         x_raw.append(load_rows("x_raw1", x[span(1), :]))
-        up_raw = [load_rows("up_raw%d" % g, up[:, span(g)]) for g in range(GROUPS)]
+        w4_words_raw = sbuf("w4_words_raw", [P, K_PASSES, FP4_BYTES * M], U8)
+        nc.sync.dma_start(
+            out=w4_words_raw[:].bitcast(I32), in_=w4_words.rearrange("a p c -> p a c").bitcast(I32)
+        )
+        up_raw = [load_rows("up_raw%d" % g, up[:, span(g)])[:] for g in range(GROUPS)]
 
         def operand(name):
             rounded = sbuf(name + "_rounded", [P, SPAN, PACK], BF16)
@@ -98,22 +93,17 @@ def tile_mix_lowrank_fm_pl_gelu_kernel(
         up_mx = [operand("up%d" % g) for g in range(GROUPS)]
         h_mx = operand("h")
 
-        def round_plain(copy, rounded, raw, cols):
+        def round_plain(copy, mx, raw, cols=span(0)):
             copy(
-                out=rounded[:, cols, :].rearrange("p (c i) j -> p c j i", i=PACK),
+                out=mx[0][:, cols, :].rearrange("p (c i) j -> p c j i", i=PACK),
                 in_=raw[:, :, cols].rearrange("p j (c i) -> p c j i", i=PACK),
             )
 
-        def round_dealt(copy, rounded, raw, cols):
-            dealt = rounded[:].rearrange("p (s m) j -> p m j s", s=PACK)
+        def round_dealt(copy, mx, raw, tiles=slice(0, PACK)):
             copy(
-                out=dealt[:, cols.start // PACK : cols.stop // PACK, :, :],
-                in_=raw[:, :, cols].rearrange("p j (m s) -> p m j s", s=PACK),
+                out=mx[0][:].rearrange("p (s m) j -> p m j s", s=PACK)[:, :, :, tiles],
+                in_=raw.rearrange("p j (m s) -> p m j s", s=PACK)[:, :, :, tiles],
             )
-
-        def round_shared(rounder, rounded, raw, vector_cols):
-            rounder(nc.scalar.copy, rounded, raw, slice(vector_cols, SPAN))
-            rounder(nc.vector.tensor_copy, rounded, raw, slice(0, vector_cols))
 
         def quantise(mx, cols=span(0)):
             rounded, words, scales = mx
@@ -123,20 +113,25 @@ def tile_mix_lowrank_fm_pl_gelu_kernel(
                 in_=rounded[:, cols, :].rearrange("p c j -> p (c j)"),
             )
 
-        w4_words_dealt = [sbuf("w4_words_dealt%d" % a, [P, FP4_BYTES * M], U8) for a in range(K_PASSES)]
-        w4_scales_dealt = [sbuf("w4_scales_dealt%d" % a, [P, M], U8) for a in range(K_PASSES)]
+        on_vector = nc.vector.tensor_copy
+        on_scalar = nc.scalar.copy
+        tile_pairs = [part(u, 2) for u in range(2)]
+        col_halves = [part(u, SPAN // 2) for u in range(2)]
 
-        def deal_w4_words(a):
-            nc.vector.tensor_copy(
-                out=w4_words_dealt[a][:].rearrange("p (g s m e) -> p g s m e", g=GROUPS, s=PACK, e=FP4_BYTES),
-                in_=w4_words_raw[a][:].rearrange("p (g m s e) -> p g s m e", g=GROUPS, s=PACK, e=FP4_BYTES),
+        w4_words_dealt = [sbuf("w4_words_dealt%d" % g, [P, K_PASSES, SPAN], U16) for g in range(GROUPS)]
+        w4_scales_dealt = [sbuf("w4_scales_dealt%d" % g, [P, K_PASSES, SPAN], U8) for g in range(GROUPS)]
+
+        def deal(dealt, raw):
+            on_vector(
+                out=dealt[:].rearrange("p a (s m) -> p a s m", s=PACK),
+                in_=raw.rearrange("p a (m s) -> p a s m", s=PACK),
             )
 
-        def deal_w4_scales(a):
-            nc.vector.tensor_copy(
-                out=w4_scales_dealt[a][:].rearrange("p (g s m) -> p g s m", g=GROUPS, s=PACK),
-                in_=w4_scales_raw[:, a, :].rearrange("p (g m s) -> p g s m", g=GROUPS, s=PACK),
-            )
+        def deal_w4_words(g):
+            deal(w4_words_dealt[g], w4_words_raw[:].bitcast(U16)[:, :, span(g)])
+
+        def deal_w4_scales(g):
+            deal(w4_scales_dealt[g], w4_scales_raw[:, :, span(g)])
 
         h_psum = [bank(PACK + tb, [P, PACK, P]) for tb in range(PACK)]
 
@@ -152,20 +147,28 @@ def tile_mix_lowrank_fm_pl_gelu_kernel(
                     stop=(a == K_PASSES - 1 and s == PACK - 1),
                 )
 
+        def round_h(copy, tb):
+            copy(out=h_mx[0][:, block(tb), :], in_=h_psum[tb][:].rearrange("p s t -> p t s"))
+
         y_psum = {}
 
         def w4_pass(i, a):
+            g, s = divmod(i, PACK)
             if a == 0:
                 y_psum[i] = bank(i, [P, T])
             nc.tensor.matmul_mx(
                 out=y_psum[i][:],
-                lhsT=w4_words_dealt[a][:, FP4_BYTES * P * i : FP4_BYTES * P * (i + 1)].bitcast(FP4X4),
-                lhsT_scale=w4_scales_dealt[a][:, block(i)],
+                lhsT=w4_words_dealt[g][:, a, block(s)].bitcast(FP4X4),
+                lhsT_scale=w4_scales_dealt[g][:, a, block(s)],
                 rhs=x_mx[a][1][:].bitcast(FP8X4),
                 rhs_scale=x_mx[a][2][:],
                 start=(a == 0),
                 stop=False,
             )
+
+        def w4_passes(i):
+            for a in range(K_PASSES):
+                w4_pass(i, a)
 
         result = [sbuf("result%d" % g, [P, PACK, T], F32) for g in range(GROUPS)]
         result_scales = sbuf("result_scales", [P, T], U8)
@@ -178,100 +181,115 @@ def tile_mix_lowrank_fm_pl_gelu_kernel(
             for g in range(GROUPS)
         ]
 
-        def finish_tile(i):
-            g, s = divmod(i, PACK)
-            nc.tensor.matmul_mx(
-                out=y_psum[i][:],
-                lhsT=up_mx[g][1][:, block(s)].bitcast(FP8X4),
-                lhsT_scale=up_mx[g][2][:, block(s)],
-                rhs=h_mx[1][:].bitcast(FP8X4),
-                rhs_scale=h_mx[2][:],
-                start=False,
-                stop=True,
-            )
-            nc.scalar.activation(out=result[g][:, s, :], in_=y_psum[i][:], func=GELU, bias=bias[:, s, g : g + 1])
+        def finish_pair(g, u):
+            for s in range(2 * u, 2 * u + 2):
+                i = PACK * g + s
+                nc.tensor.matmul_mx(
+                    out=y_psum[i][:],
+                    lhsT=up_mx[g][1][:, block(s)].bitcast(FP8X4),
+                    lhsT_scale=up_mx[g][2][:, block(s)],
+                    rhs=h_mx[1][:].bitcast(FP8X4),
+                    rhs_scale=h_mx[2][:],
+                    start=False,
+                    stop=True,
+                )
+                nc.scalar.activation(out=result[g][:, s, :], in_=y_psum[i][:], func=GELU, bias=bias[:, s, g : g + 1])
 
-        def store_pair(g, s):
+        def store_result(g, tiles=slice(0, PACK)):
             rows = out_0[span(g), :].rearrange("(p s) t -> p s t", s=PACK)
-            nc.sync.dma_start(out=rows[:, s : s + 2, :], in_=result[g][:, s : s + 2, :])
+            nc.sync.dma_start(out=rows[:, tiles, :], in_=result[g][:, tiles, :])
 
         def store_words(g):
             nc.sync.dma_start(
                 out=out_1[g].rearrange("p t i -> p (t i)").bitcast(I32), in_=result_mx[g][1][:].bitcast(I32)
             )
 
-        def round_on_vector(rounder, mx, raw):
-            rounder(nc.vector.tensor_copy, mx[0], raw, span(0))
+        def round_up(copy, g, u):
+            round_dealt(copy, up_mx[g], up_raw[g], tile_pairs[u])
 
-        deal_w4_words(0)
-        round_shared(round_plain, x_mx[0][0], x_raw[0], VECTOR_COLS_X0)
+        def quantise_up(g, u):
+            quantise(up_mx[g], col_halves[u])
+
+        round_plain(on_scalar, x_mx[0], x_raw[0])
+        for g in range(GROUPS):
+            deal_w4_scales(g)
         bias_psum = bank(0, [P, PACK, P])
         for s in range(PACK):
             nc.tensor.transpose(bias_psum[:, s, :], bias_rows[:, s:SPAN:PACK], identity[:])
         bias = sbuf("bias", [P, PACK, GROUPS], F32)
-        nc.scalar.copy(out=bias[:], in_=bias_psum[:, :, BIAS_ROW:P:QUADRANT])
-        deal_w4_scales(0)
+        on_scalar(out=bias[:], in_=bias_psum[:, :, BIAS_ROW:P:QUADRANT])
+        round_dealt(on_vector, down_mx[0], down_raw[0][:])
         quantise(x_mx[0])
-        for i in range(BANKS - PACK):
-            w4_pass(i, 0)
-        round_dealt(nc.scalar.copy, down_mx[0][0], down_raw[0], span(0))
-        deal_w4_scales(1)
-        deal_w4_words(1)
         quantise(down_mx[0])
         for tb in range(PACK):
             h_passes(0, tb)
 
-        round_shared(round_dealt, down_mx[1][0], down_raw[1], VECTOR_COLS_DOWN1)
+        round_dealt(on_scalar, down_mx[1], down_raw[1][:], tile_pairs[1])
+        round_dealt(on_vector, down_mx[1], down_raw[1][:], tile_pairs[0])
         quantise(down_mx[1])
-        round_plain(nc.scalar.copy, x_mx[1][0], x_raw[1], block(PACK - 1))
-        round_plain(nc.vector.tensor_copy, x_mx[1][0], x_raw[1], block(0))
+        round_plain(on_scalar, x_mx[1], x_raw[1], block(PACK - 1))
+        round_plain(on_vector, x_mx[1], x_raw[1], block(0))
         for tb in range(PACK):
             if tb + 1 < PACK - 1:
-                round_plain(nc.vector.tensor_copy, x_mx[1][0], x_raw[1], block(tb + 1))
+                round_plain(on_vector, x_mx[1], x_raw[1], block(tb + 1))
             quantise(x_mx[1], block(tb))
             h_passes(1, tb)
-            nc.scalar.copy(out=h_mx[0][:, block(tb), :], in_=h_psum[tb][:].rearrange("p s t -> p t s"))
-        for i in range(BANKS - PACK):
-            w4_pass(i, 1)
-        round_on_vector(round_dealt, up_mx[0], up_raw[0])
-        quantise(h_mx, slice(0, T // 2))
-        quantise(up_mx[0])
-        quantise(h_mx, slice(T // 2, T))
-        for i in range(BANKS - PACK, EARLY_TILES):
-            for a in range(K_PASSES):
-                w4_pass(i, a)
-        round_on_vector(round_dealt, up_mx[1], up_raw[1])
-        quantise(up_mx[1])
+            round_h(on_scalar, tb)
+        for g in range(GROUPS - 1):
+            deal_w4_words(g)
+        quantise(h_mx)
 
-        late_passes = [(i, a) for i in range(EARLY_TILES, TILES) for a in range(K_PASSES)]
-        issued = 0
-        for i in range(TILES):
-            g, s = divmod(i, PACK)
-            finish_tile(i)
-            due = min(len(late_passes), (i + 1) * len(late_passes) // (TILES - 1))
-            for late in late_passes[issued:due]:
-                w4_pass(*late)
-            issued = due
-            if s % 2 == 1:
-                store_pair(g, s - 1)
-            if s == PACK - 1 and g == 0:
-                round_on_vector(round_dealt, up_mx[2], up_raw[2])
-                quantise(up_mx[2])
-                round_on_vector(round_plain, result_mx[0], result[0])
-                round_on_vector(round_dealt, up_mx[3], up_raw[3])
-                quantise(up_mx[3])
-                quantise(result_mx[0])
-            if s == PACK - 1 and g == GROUPS - 2:
-                store_words(0)
-                for middle in range(1, GROUPS - 1):
-                    round_on_vector(round_plain, result_mx[middle], result[middle])
-                for middle in range(1, GROUPS - 1):
-                    quantise(result_mx[middle])
-        for middle in range(1, GROUPS - 1):
-            store_words(middle)
-        round_shared(round_plain, result_mx[GROUPS - 1][0], result[GROUPS - 1], VECTOR_COLS_LAST)
-        quantise(result_mx[GROUPS - 1])
-        store_words(GROUPS - 1)
+        late_tiles = list(range(TILES))
+
+        def w4_tiles(count):
+            for i in late_tiles[:count]:
+                w4_passes(i)
+                late_tiles.remove(i)
+
+        def finish_and_refill(g, u):
+            finish_pair(g, u)
+            w4_tiles(u + 1)
+            if u == 1:
+                store_result(g)
+
+        w4_tiles(EARLY_TILES)
+        round_up(on_vector, 0, 0)
+        deal_w4_words(GROUPS - 1)
+        quantise_up(0, 0)
+        finish_and_refill(0, 0)
+        round_up(on_vector, 0, 1)
+        quantise_up(0, 1)
+        finish_and_refill(0, 1)
+        for u in range(2):
+            round_up(on_vector, 1, u)
+        for u in range(2):
+            quantise_up(1, u)
+            finish_and_refill(1, u)
+        round_plain(on_vector, result_mx[0], result[0])
+        for u in range(2):
+            round_up(on_vector, 2, u)
+        quantise_up(2, 0)
+        finish_and_refill(2, 0)
+        quantise_up(2, 1)
+        quantise(result_mx[0])
+        store_words(0)
+        finish_and_refill(2, 1)
+        for u in range(2):
+            round_up(on_vector, 3, u)
+        quantise_up(3, 0)
+        finish_and_refill(3, 0)
+        round_plain(on_vector, result_mx[1], result[1])
+        quantise_up(3, 1)
+        quantise(result_mx[1])
+        store_words(1)
+        finish_and_refill(3, 1)
+        round_plain(on_vector, result_mx[2], result[2])
+        quantise(result_mx[2])
+        store_words(2)
+        round_plain(on_scalar, result_mx[3], result[3], slice(VECTOR_COLS_LAST, T))
+        round_plain(on_vector, result_mx[3], result[3], slice(0, VECTOR_COLS_LAST))
+        quantise(result_mx[3])
+        store_words(3)
         for q in range(P // QUADRANT):
             nc.scalar.dma_start(
                 out=out_2[:, PACK * q : PACK * (q + 1), :].bitcast(I32),

@@ -27,8 +27,7 @@ TILES = M // P
 BIAS_ROW = 8
 BANKS = 8
 
-VECTOR_COLS_LAST = 288
-EARLY_TILES = 6
+VECTOR_COLS_LAST = 192
 
 
 def tile_mix_lowrank_fm_pl_gelu_kernel(
@@ -62,10 +61,22 @@ def tile_mix_lowrank_fm_pl_gelu_kernel(
         identity = sbuf("identity", [P, P], F32)
         make_identity(nc, identity[:])
 
+        warm = sbuf("warm", [P, 2], F32)
+        nc.vector.memset(warm[:, 0:1], 0.0)
+        nc.scalar.activation(out=warm[:, 1:2], in_=warm[:, 0:1], func=GELU)
+
         def load_rows(name, rows):
             raw = sbuf(name, [P, PACK, rows.shape[1]], F32)
             nc.sync.dma_start(out=raw[:], in_=rows.rearrange("(p j) c -> p j c", j=PACK))
             return raw
+
+        def load_w4_words(name, groups):
+            cols = slice(FP4_BYTES * SPAN * groups.start, FP4_BYTES * SPAN * groups.stop)
+            raw = sbuf(name, [P, K_PASSES, cols.stop - cols.start], U8)
+            nc.sync.dma_start(
+                out=raw[:].bitcast(I32), in_=w4_words[:, :, cols].rearrange("a p c -> p a c").bitcast(I32)
+            )
+            return [raw[:].bitcast(U16)[:, :, span(u)] for u in range(len(groups))]
 
         x_raw = [load_rows("x_raw0", x[span(0), :])]
         for r in range(PACK):
@@ -74,12 +85,10 @@ def tile_mix_lowrank_fm_pl_gelu_kernel(
                 in_=w4_scales.rearrange("a (q r) n -> r q a n", r=PACK)[r].bitcast(I32),
             )
         nc.sync.dma_start(out=bias_rows[BIAS_ROW:P:QUADRANT, :], in_=b.rearrange("(g c) -> g c", g=GROUPS))
-        down_raw = [load_rows("down_raw%d" % a, down[span(a), :]) for a in range(K_PASSES)]
+        w4_words_raw = load_w4_words("w4_words_first", range(0, 1))
         x_raw.append(load_rows("x_raw1", x[span(1), :]))
-        w4_words_raw = sbuf("w4_words_raw", [P, K_PASSES, FP4_BYTES * M], U8)
-        nc.sync.dma_start(
-            out=w4_words_raw[:].bitcast(I32), in_=w4_words.rearrange("a p c -> p a c").bitcast(I32)
-        )
+        down_raw = [load_rows("down_raw%d" % a, down[span(a), :]) for a in range(K_PASSES)]
+        w4_words_raw.extend(load_w4_words("w4_words_rest", range(1, GROUPS)))
         up_raw = [load_rows("up_raw%d" % g, up[:, span(g)])[:] for g in range(GROUPS)]
 
         def operand(name):
@@ -128,15 +137,15 @@ def tile_mix_lowrank_fm_pl_gelu_kernel(
             )
 
         def deal_w4_words(g):
-            deal(w4_words_dealt[g], w4_words_raw[:].bitcast(U16)[:, :, span(g)])
+            deal(w4_words_dealt[g], w4_words_raw[g])
 
         def deal_w4_scales(g):
             deal(w4_scales_dealt[g], w4_scales_raw[:, :, span(g)])
 
         h_psum = [bank(PACK + tb, [P, PACK, P]) for tb in range(PACK)]
 
-        def h_passes(a, tb):
-            for s in range(PACK):
+        def h_passes(a, tb, tiles=range(PACK)):
+            for s in tiles:
                 nc.tensor.matmul_mx(
                     out=h_psum[tb][:, s, :],
                     lhsT=down_mx[a][1][:, block(s)].bitcast(FP8X4),
@@ -213,81 +222,73 @@ def tile_mix_lowrank_fm_pl_gelu_kernel(
         round_plain(on_scalar, x_mx[0], x_raw[0])
         for g in range(GROUPS):
             deal_w4_scales(g)
+        deal_w4_words(0)
         bias_psum = bank(0, [P, PACK, P])
         for s in range(PACK):
             nc.tensor.transpose(bias_psum[:, s, :], bias_rows[:, s:SPAN:PACK], identity[:])
         bias = sbuf("bias", [P, PACK, GROUPS], F32)
         on_scalar(out=bias[:], in_=bias_psum[:, :, BIAS_ROW:P:QUADRANT])
-        round_dealt(on_vector, down_mx[0], down_raw[0][:])
         quantise(x_mx[0])
-        quantise(down_mx[0])
-        for tb in range(PACK):
-            h_passes(0, tb)
+        round_plain(on_scalar, x_mx[1], x_raw[1], col_halves[1])
+        round_plain(on_vector, x_mx[1], x_raw[1], col_halves[0])
+        quantise(x_mx[1])
+        for a in range(K_PASSES):
+            for i in range(PACK):
+                w4_pass(i, a)
 
-        round_dealt(on_scalar, down_mx[1], down_raw[1][:], tile_pairs[1])
-        round_dealt(on_vector, down_mx[1], down_raw[1][:], tile_pairs[0])
-        quantise(down_mx[1])
-        round_plain(on_scalar, x_mx[1], x_raw[1], block(PACK - 1))
-        round_plain(on_vector, x_mx[1], x_raw[1], block(0))
+        for a in range(K_PASSES):
+            round_dealt(on_scalar, down_mx[a], down_raw[a][:], tile_pairs[1])
+            round_dealt(on_vector, down_mx[a], down_raw[a][:], tile_pairs[0])
+            for u in range(2):
+                quantise(down_mx[a], col_halves[u])
+                for tb in range(PACK):
+                    h_passes(a, tb, range(2 * u, 2 * u + 2))
         for tb in range(PACK):
-            if tb + 1 < PACK - 1:
-                round_plain(on_vector, x_mx[1], x_raw[1], block(tb + 1))
-            quantise(x_mx[1], block(tb))
-            h_passes(1, tb)
             round_h(on_scalar, tb)
-        for g in range(GROUPS - 1):
+        for g in range(1, GROUPS):
             deal_w4_words(g)
-        quantise(h_mx)
+        for i in range(PACK, BANKS):
+            w4_passes(i)
 
-        late_tiles = list(range(TILES))
+        late_tiles = range(BANKS, TILES)
+        gaps = TILES // 2 - 2
 
-        def w4_tiles(count):
-            for i in late_tiles[:count]:
-                w4_passes(i)
-                late_tiles.remove(i)
+        def late_tiles_due(pair):
+            return -(-len(late_tiles) * min(pair, gaps) // gaps)
 
         def finish_and_refill(g, u):
             finish_pair(g, u)
-            w4_tiles(u + 1)
-            if u == 1:
-                store_result(g)
+            store_result(g, tile_pairs[u])
+            pair = 2 * g + u
+            for i in late_tiles[late_tiles_due(max(pair - 1, 0)) : late_tiles_due(pair)]:
+                w4_passes(i)
 
-        w4_tiles(EARLY_TILES)
         round_up(on_vector, 0, 0)
-        deal_w4_words(GROUPS - 1)
+        quantise(h_mx, col_halves[0])
         quantise_up(0, 0)
+        quantise(h_mx, col_halves[1])
         finish_and_refill(0, 0)
         round_up(on_vector, 0, 1)
         quantise_up(0, 1)
         finish_and_refill(0, 1)
-        for u in range(2):
-            round_up(on_vector, 1, u)
-        for u in range(2):
-            quantise_up(1, u)
-            finish_and_refill(1, u)
-        round_plain(on_vector, result_mx[0], result[0])
-        for u in range(2):
-            round_up(on_vector, 2, u)
-        quantise_up(2, 0)
-        finish_and_refill(2, 0)
-        quantise_up(2, 1)
-        quantise(result_mx[0])
-        store_words(0)
-        finish_and_refill(2, 1)
-        for u in range(2):
-            round_up(on_vector, 3, u)
-        quantise_up(3, 0)
-        finish_and_refill(3, 0)
-        round_plain(on_vector, result_mx[1], result[1])
-        quantise_up(3, 1)
+        for g in range(1, GROUPS):
+            for u in range(2):
+                round_up(on_vector, g, u)
+                if g > 1:
+                    round_plain(on_vector, result_mx[0], result[0], block(2 * (g - 2) + u))
+                quantise_up(g, u)
+                if (g, u) == (GROUPS - 1, 1):
+                    round_plain(on_vector, result_mx[1], result[1])
+                    quantise(result_mx[0])
+                    store_words(0)
+                finish_and_refill(g, u)
+        round_plain(on_vector, result_mx[2], result[2])
         quantise(result_mx[1])
         store_words(1)
-        finish_and_refill(3, 1)
-        round_plain(on_vector, result_mx[2], result[2])
-        quantise(result_mx[2])
-        store_words(2)
         round_plain(on_scalar, result_mx[3], result[3], slice(VECTOR_COLS_LAST, T))
         round_plain(on_vector, result_mx[3], result[3], slice(0, VECTOR_COLS_LAST))
+        quantise(result_mx[2])
+        store_words(2)
         quantise(result_mx[3])
         store_words(3)
         for q in range(P // QUADRANT):

@@ -132,8 +132,8 @@ def tile_mix_lowrank_fm_pl_gelu_kernel(
 
         def deal(dealt, raw):
             on_vector(
-                out=dealt[:].rearrange("p a (s m) -> p a s m", s=PACK),
-                in_=raw.rearrange("p a (m s) -> p a s m", s=PACK),
+                out=dealt[:].rearrange("p a (s m) -> p a m s", s=PACK),
+                in_=raw.rearrange("p a (m s) -> p a m s", s=PACK),
             )
 
         def deal_w4_words(g):
@@ -181,10 +181,11 @@ def tile_mix_lowrank_fm_pl_gelu_kernel(
 
         result = [sbuf("result%d" % g, [P, PACK, T], F32) for g in range(GROUPS)]
         result_scales = sbuf("result_scales", [P, T], U8)
+        result_words = sbuf("result_words", [P, GROUPS, T], U32)
         result_mx = [
             (
                 sbuf("result_rounded%d" % g, [P, T, PACK], BF16),
-                sbuf("result_words%d" % g, [P, T], U32),
+                result_words[:, g, :],
                 result_scales[PACK * g : P, :],
             )
             for g in range(GROUPS)
@@ -208,9 +209,10 @@ def tile_mix_lowrank_fm_pl_gelu_kernel(
             rows = out_0[span(g), :].rearrange("(p s) t -> p s t", s=PACK)
             nc.sync.dma_start(out=rows[:, tiles, :], in_=result[g][:, tiles, :])
 
-        def store_words(g):
+        def store_words(groups):
             nc.sync.dma_start(
-                out=out_1[g].rearrange("p t i -> p (t i)").bitcast(I32), in_=result_mx[g][1][:].bitcast(I32)
+                out=out_1[groups].rearrange("g p t i -> p g (t i)").bitcast(I32),
+                in_=result_words[:, groups, :].bitcast(I32),
             )
 
         def round_up(copy, g, u):
@@ -251,16 +253,16 @@ def tile_mix_lowrank_fm_pl_gelu_kernel(
             w4_passes(i)
 
         late_tiles = range(BANKS, TILES)
-        gaps = TILES // 2 - 2
 
         def late_tiles_due(pair):
-            return -(-len(late_tiles) * min(pair, gaps) // gaps)
+            return min(len(late_tiles), max(0, pair, 2 * (pair + 2) - BANKS))
 
         def finish_and_refill(g, u):
             finish_pair(g, u)
-            store_result(g, tile_pairs[u])
+            if u == 1 and g < GROUPS - 1:
+                store_result(g)
             pair = 2 * g + u
-            for i in late_tiles[late_tiles_due(max(pair - 1, 0)) : late_tiles_due(pair)]:
+            for i in late_tiles[late_tiles_due(pair - 1) : late_tiles_due(pair)]:
                 w4_passes(i)
 
         round_up(on_vector, 0, 0)
@@ -271,26 +273,35 @@ def tile_mix_lowrank_fm_pl_gelu_kernel(
         round_up(on_vector, 0, 1)
         quantise_up(0, 1)
         finish_and_refill(0, 1)
-        for g in range(1, GROUPS):
-            for u in range(2):
-                round_up(on_vector, g, u)
-                if g > 1:
-                    round_plain(on_vector, result_mx[0], result[0], block(2 * (g - 2) + u))
-                quantise_up(g, u)
-                if (g, u) == (GROUPS - 1, 1):
-                    round_plain(on_vector, result_mx[1], result[1])
-                    quantise(result_mx[0])
-                    store_words(0)
-                finish_and_refill(g, u)
-        round_plain(on_vector, result_mx[2], result[2])
+        for u in range(2):
+            round_up(on_vector, 1, u)
+            quantise_up(1, u)
+            finish_and_refill(1, u)
+        for u in range(2):
+            round_up(on_vector, 2, u)
+            round_plain(on_vector, result_mx[0], result[0], block(u))
+            quantise_up(2, u)
+            finish_and_refill(2, u)
+        round_up(on_vector, 3, 0)
+        round_plain(on_vector, result_mx[0], result[0], col_halves[1])
+        quantise_up(3, 0)
+        finish_and_refill(3, 0)
+        round_up(on_vector, 3, 1)
+        quantise(result_mx[0])
+        quantise_up(3, 1)
+        finish_and_refill(3, 1)
+        store_words(slice(0, 1))
+        for u in range(2):
+            store_result(GROUPS - 1, tile_pairs[u])
+        for g in range(1, 3):
+            round_plain(on_vector, result_mx[g], result[g])
         quantise(result_mx[1])
-        store_words(1)
         round_plain(on_scalar, result_mx[3], result[3], slice(VECTOR_COLS_LAST, T))
         round_plain(on_vector, result_mx[3], result[3], slice(0, VECTOR_COLS_LAST))
         quantise(result_mx[2])
-        store_words(2)
+        store_words(slice(1, 3))
         quantise(result_mx[3])
-        store_words(3)
+        store_words(slice(3, 4))
         for q in range(P // QUADRANT):
             nc.scalar.dma_start(
                 out=out_2[:, PACK * q : PACK * (q + 1), :].bitcast(I32),

@@ -27,7 +27,7 @@ TILES = M // P
 BIAS_ROW = 8
 BANKS = 8
 
-VECTOR_COLS_LAST = 192
+VECTOR_COLS_LAST = 96
 
 
 def tile_mix_lowrank_fm_pl_gelu_kernel(
@@ -245,17 +245,17 @@ def tile_mix_lowrank_fm_pl_gelu_kernel(
                 quantise(down_mx[a], col_halves[u])
                 for tb in range(PACK):
                     h_passes(a, tb, range(2 * u, 2 * u + 2))
+        deal_w4_words(1)
         for tb in range(PACK):
-            round_h(on_scalar, tb)
-        for g in range(1, GROUPS):
-            deal_w4_words(g)
+            round_h(on_vector if tb == 1 else on_scalar, tb)
+        deal_w4_words(2)
         for i in range(PACK, BANKS):
             w4_passes(i)
 
         late_tiles = range(BANKS, TILES)
 
         def late_tiles_due(pair):
-            return min(len(late_tiles), max(0, pair, 2 * (pair + 2) - BANKS))
+            return 0 if pair < 1 else min(len(late_tiles), max(pair + 1, 2 * (pair + 2) - BANKS))
 
         def finish_and_refill(g, u):
             finish_pair(g, u)
@@ -265,12 +265,13 @@ def tile_mix_lowrank_fm_pl_gelu_kernel(
             for i in late_tiles[late_tiles_due(pair - 1) : late_tiles_due(pair)]:
                 w4_passes(i)
 
-        round_up(on_vector, 0, 0)
         quantise(h_mx, col_halves[0])
-        quantise_up(0, 0)
+        round_up(on_scalar, 0, 1)
+        round_up(on_vector, 0, 0)
         quantise(h_mx, col_halves[1])
+        quantise_up(0, 0)
         finish_and_refill(0, 0)
-        round_up(on_vector, 0, 1)
+        deal_w4_words(3)
         quantise_up(0, 1)
         finish_and_refill(0, 1)
         for u in range(2):
@@ -282,17 +283,14 @@ def tile_mix_lowrank_fm_pl_gelu_kernel(
             round_plain(on_vector, result_mx[0], result[0], block(u))
             quantise_up(2, u)
             finish_and_refill(2, u)
-        round_up(on_vector, 3, 0)
-        round_plain(on_vector, result_mx[0], result[0], col_halves[1])
-        quantise_up(3, 0)
-        finish_and_refill(3, 0)
-        round_up(on_vector, 3, 1)
-        quantise(result_mx[0])
-        quantise_up(3, 1)
-        finish_and_refill(3, 1)
-        store_words(slice(0, 1))
         for u in range(2):
-            store_result(GROUPS - 1, tile_pairs[u])
+            round_up(on_vector, 3, u)
+            round_plain(on_vector, result_mx[0], result[0], block(2 + u))
+            quantise_up(3, u)
+            finish_and_refill(3, u)
+        quantise(result_mx[0])
+        store_words(slice(0, 1))
+        store_result(GROUPS - 1)
         for g in range(1, 3):
             round_plain(on_vector, result_mx[g], result[g])
         quantise(result_mx[1])

@@ -27,7 +27,11 @@ TILES = M // P
 BIAS_ROW = 8
 BANKS = 8
 
-VECTOR_COLS_LAST = 96
+VECTOR_COLS_DOWN = 368
+VECTOR_COLS_X1 = 256
+VECTOR_COLS_UP0 = 448
+VECTOR_COLS_LAST = 288
+DOUBLE_REFILL = (1, 5)
 
 
 def tile_mix_lowrank_fm_pl_gelu_kernel(
@@ -108,11 +112,16 @@ def tile_mix_lowrank_fm_pl_gelu_kernel(
                 in_=raw[:, :, cols].rearrange("p j (c i) -> p c j i", i=PACK),
             )
 
-        def round_dealt(copy, mx, raw, tiles=slice(0, PACK)):
+        def round_dealt(copy, mx, raw, cols=span(0)):
+            dealt = mx[0][:].rearrange("p (s m) j -> p m j s", s=PACK)
             copy(
-                out=mx[0][:].rearrange("p (s m) j -> p m j s", s=PACK)[:, :, :, tiles],
-                in_=raw.rearrange("p j (m s) -> p m j s", s=PACK)[:, :, :, tiles],
+                out=dealt[:, cols.start // PACK : cols.stop // PACK, :, :],
+                in_=raw[:, :, cols].rearrange("p j (m s) -> p m j s", s=PACK),
             )
+
+        def round_shared(rounder, mx, raw, vector_cols):
+            rounder(nc.scalar.copy, mx, raw, slice(vector_cols, SPAN))
+            rounder(nc.vector.tensor_copy, mx, raw, slice(0, vector_cols))
 
         def quantise(mx, cols=span(0)):
             rounded, words, scales = mx
@@ -144,8 +153,8 @@ def tile_mix_lowrank_fm_pl_gelu_kernel(
 
         h_psum = [bank(PACK + tb, [P, PACK, P]) for tb in range(PACK)]
 
-        def h_passes(a, tb, tiles=range(PACK)):
-            for s in tiles:
+        def h_passes(a, tb):
+            for s in range(PACK):
                 nc.tensor.matmul_mx(
                     out=h_psum[tb][:, s, :],
                     lhsT=down_mx[a][1][:, block(s)].bitcast(FP8X4),
@@ -215,9 +224,6 @@ def tile_mix_lowrank_fm_pl_gelu_kernel(
                 in_=result_words[:, groups, :].bitcast(I32),
             )
 
-        def round_up(copy, g, u):
-            round_dealt(copy, up_mx[g], up_raw[g], tile_pairs[u])
-
         def quantise_up(g, u):
             quantise(up_mx[g], col_halves[u])
 
@@ -231,71 +237,61 @@ def tile_mix_lowrank_fm_pl_gelu_kernel(
         bias = sbuf("bias", [P, PACK, GROUPS], F32)
         on_scalar(out=bias[:], in_=bias_psum[:, :, BIAS_ROW:P:QUADRANT])
         quantise(x_mx[0])
-        round_plain(on_scalar, x_mx[1], x_raw[1], col_halves[1])
-        round_plain(on_vector, x_mx[1], x_raw[1], col_halves[0])
+        round_shared(round_plain, x_mx[1], x_raw[1], VECTOR_COLS_X1)
         quantise(x_mx[1])
         for a in range(K_PASSES):
             for i in range(PACK):
                 w4_pass(i, a)
 
         for a in range(K_PASSES):
-            round_dealt(on_scalar, down_mx[a], down_raw[a][:], tile_pairs[1])
-            round_dealt(on_vector, down_mx[a], down_raw[a][:], tile_pairs[0])
-            for u in range(2):
-                quantise(down_mx[a], col_halves[u])
-                for tb in range(PACK):
-                    h_passes(a, tb, range(2 * u, 2 * u + 2))
-        deal_w4_words(1)
+            round_shared(round_dealt, down_mx[a], down_raw[a], VECTOR_COLS_DOWN)
+            quantise(down_mx[a])
+            for tb in range(PACK):
+                h_passes(a, tb)
         for tb in range(PACK):
-            round_h(on_vector if tb == 1 else on_scalar, tb)
-        deal_w4_words(2)
+            round_h(on_scalar, tb)
+        for g in range(1, GROUPS):
+            deal_w4_words(g)
         for i in range(PACK, BANKS):
             w4_passes(i)
 
-        late_tiles = range(BANKS, TILES)
-
-        def late_tiles_due(pair):
-            return 0 if pair < 1 else min(len(late_tiles), max(pair + 1, 2 * (pair + 2) - BANKS))
+        late_tiles = list(range(BANKS, TILES))
 
         def finish_and_refill(g, u):
             finish_pair(g, u)
-            if u == 1 and g < GROUPS - 1:
-                store_result(g)
+            if g < GROUPS - 1:
+                store_result(g, tile_pairs[u])
             pair = 2 * g + u
-            for i in late_tiles[late_tiles_due(pair - 1) : late_tiles_due(pair)]:
+            count = 0 if pair == 0 else 2 if pair in DOUBLE_REFILL else 1
+            for i in late_tiles[:count]:
                 w4_passes(i)
+                late_tiles.remove(i)
+
+        def finish_group(g):
+            for u in range(2):
+                quantise_up(g, u)
+                finish_and_refill(g, u)
 
         quantise(h_mx, col_halves[0])
-        round_up(on_scalar, 0, 1)
-        round_up(on_vector, 0, 0)
+        round_shared(round_dealt, up_mx[0], up_raw[0], VECTOR_COLS_UP0)
         quantise(h_mx, col_halves[1])
-        quantise_up(0, 0)
-        finish_and_refill(0, 0)
-        deal_w4_words(3)
-        quantise_up(0, 1)
-        finish_and_refill(0, 1)
-        for u in range(2):
-            round_up(on_vector, 1, u)
-            quantise_up(1, u)
-            finish_and_refill(1, u)
-        for u in range(2):
-            round_up(on_vector, 2, u)
-            round_plain(on_vector, result_mx[0], result[0], block(u))
-            quantise_up(2, u)
-            finish_and_refill(2, u)
-        for u in range(2):
-            round_up(on_vector, 3, u)
-            round_plain(on_vector, result_mx[0], result[0], block(2 + u))
-            quantise_up(3, u)
-            finish_and_refill(3, u)
+        finish_group(0)
+        round_dealt(on_vector, up_mx[1], up_raw[1])
+        finish_group(1)
+        round_dealt(on_vector, up_mx[2], up_raw[2])
+        round_plain(on_vector, result_mx[0], result[0], col_halves[0])
+        finish_group(2)
+        round_plain(on_vector, result_mx[0], result[0], col_halves[1])
+        round_dealt(on_vector, up_mx[3], up_raw[3])
         quantise(result_mx[0])
+        finish_group(3)
+        round_plain(on_vector, result_mx[1], result[1])
         store_words(slice(0, 1))
-        store_result(GROUPS - 1)
-        for g in range(1, 3):
-            round_plain(on_vector, result_mx[g], result[g])
+        for u in range(2):
+            store_result(3, tile_pairs[u])
+        round_plain(on_vector, result_mx[2], result[2])
         quantise(result_mx[1])
-        round_plain(on_scalar, result_mx[3], result[3], slice(VECTOR_COLS_LAST, T))
-        round_plain(on_vector, result_mx[3], result[3], slice(0, VECTOR_COLS_LAST))
+        round_shared(round_plain, result_mx[3], result[3], VECTOR_COLS_LAST)
         quantise(result_mx[2])
         store_words(slice(1, 3))
         quantise(result_mx[3])

@@ -28,10 +28,10 @@ BIAS_ROW = 8
 BANKS = 8
 
 VECTOR_COLS_DOWN = 368
-VECTOR_COLS_X1 = 256
-VECTOR_COLS_UP0 = 448
+VECTOR_COLS_UP0 = 368
 VECTOR_COLS_LAST = 288
 DOUBLE_REFILL = (1, 5)
+EARLY_TILES = 7
 
 
 def tile_mix_lowrank_fm_pl_gelu_kernel(
@@ -74,13 +74,10 @@ def tile_mix_lowrank_fm_pl_gelu_kernel(
             nc.sync.dma_start(out=raw[:], in_=rows.rearrange("(p j) c -> p j c", j=PACK))
             return raw
 
-        def load_w4_words(name, groups):
-            cols = slice(FP4_BYTES * SPAN * groups.start, FP4_BYTES * SPAN * groups.stop)
-            raw = sbuf(name, [P, K_PASSES, cols.stop - cols.start], U8)
-            nc.sync.dma_start(
-                out=raw[:].bitcast(I32), in_=w4_words[:, :, cols].rearrange("a p c -> p a c").bitcast(I32)
-            )
-            return [raw[:].bitcast(U16)[:, :, span(u)] for u in range(len(groups))]
+        def load_w4_words(a):
+            raw = sbuf("w4_words_raw%d" % a, [P, FP4_BYTES * M], U8)
+            nc.sync.dma_start(out=raw[:].bitcast(I32), in_=w4_words[a].bitcast(I32))
+            return raw
 
         x_raw = [load_rows("x_raw0", x[span(0), :])]
         for r in range(PACK):
@@ -89,10 +86,10 @@ def tile_mix_lowrank_fm_pl_gelu_kernel(
                 in_=w4_scales.rearrange("a (q r) n -> r q a n", r=PACK)[r].bitcast(I32),
             )
         nc.sync.dma_start(out=bias_rows[BIAS_ROW:P:QUADRANT, :], in_=b.rearrange("(g c) -> g c", g=GROUPS))
-        w4_words_raw = load_w4_words("w4_words_first", range(0, 1))
-        x_raw.append(load_rows("x_raw1", x[span(1), :]))
+        w4_words_raw = [load_w4_words(0)]
         down_raw = [load_rows("down_raw%d" % a, down[span(a), :]) for a in range(K_PASSES)]
-        w4_words_raw.extend(load_w4_words("w4_words_rest", range(1, GROUPS)))
+        x_raw.append(load_rows("x_raw1", x[span(1), :]))
+        w4_words_raw.append(load_w4_words(1))
         up_raw = [load_rows("up_raw%d" % g, up[:, span(g)])[:] for g in range(GROUPS)]
 
         def operand(name):
@@ -136,7 +133,9 @@ def tile_mix_lowrank_fm_pl_gelu_kernel(
         tile_pairs = [part(u, 2) for u in range(2)]
         col_halves = [part(u, SPAN // 2) for u in range(2)]
 
-        w4_words_dealt = [sbuf("w4_words_dealt%d" % g, [P, K_PASSES, SPAN], U16) for g in range(GROUPS)]
+        w4_words_dealt = [
+            [sbuf("w4_words_dealt%d_%d" % (a, half), [P, 2, SPAN], U16) for half in range(2)] for a in range(K_PASSES)
+        ]
         w4_scales_dealt = [sbuf("w4_scales_dealt%d" % g, [P, K_PASSES, SPAN], U8) for g in range(GROUPS)]
 
         def deal(dealt, raw):
@@ -145,8 +144,9 @@ def tile_mix_lowrank_fm_pl_gelu_kernel(
                 in_=raw.rearrange("p a (m s) -> p a m s", s=PACK),
             )
 
-        def deal_w4_words(g):
-            deal(w4_words_dealt[g], w4_words_raw[g])
+        def deal_w4_words(a, half):
+            columns = w4_words_raw[a][:].bitcast(U16)[:, part(half, 2 * SPAN)]
+            deal(w4_words_dealt[a][half], columns.rearrange("p (g c) -> p g c", g=2))
 
         def deal_w4_scales(g):
             deal(w4_scales_dealt[g], w4_scales_raw[:, :, span(g)])
@@ -176,7 +176,7 @@ def tile_mix_lowrank_fm_pl_gelu_kernel(
                 y_psum[i] = bank(i, [P, T])
             nc.tensor.matmul_mx(
                 out=y_psum[i][:],
-                lhsT=w4_words_dealt[g][:, a, block(s)].bitcast(FP4X4),
+                lhsT=w4_words_dealt[a][g // 2][:, g % 2, block(s)].bitcast(FP4X4),
                 lhsT_scale=w4_scales_dealt[g][:, a, block(s)],
                 rhs=x_mx[a][1][:].bitcast(FP8X4),
                 rhs_scale=x_mx[a][2][:],
@@ -230,39 +230,48 @@ def tile_mix_lowrank_fm_pl_gelu_kernel(
         round_plain(on_scalar, x_mx[0], x_raw[0])
         for g in range(GROUPS):
             deal_w4_scales(g)
-        deal_w4_words(0)
+        deal_w4_words(0, 0)
         bias_psum = bank(0, [P, PACK, P])
         for s in range(PACK):
             nc.tensor.transpose(bias_psum[:, s, :], bias_rows[:, s:SPAN:PACK], identity[:])
         bias = sbuf("bias", [P, PACK, GROUPS], F32)
         on_scalar(out=bias[:], in_=bias_psum[:, :, BIAS_ROW:P:QUADRANT])
         quantise(x_mx[0])
-        round_shared(round_plain, x_mx[1], x_raw[1], VECTOR_COLS_X1)
-        quantise(x_mx[1])
-        for a in range(K_PASSES):
-            for i in range(PACK):
-                w4_pass(i, a)
-
-        for a in range(K_PASSES):
-            round_shared(round_dealt, down_mx[a], down_raw[a], VECTOR_COLS_DOWN)
-            quantise(down_mx[a])
-            for tb in range(PACK):
-                h_passes(a, tb)
+        for i in range(PACK):
+            w4_pass(i, 0)
+        round_shared(round_dealt, down_mx[0], down_raw[0], VECTOR_COLS_DOWN)
+        deal_w4_words(0, 1)
+        quantise(down_mx[0])
         for tb in range(PACK):
+            h_passes(0, tb)
+
+        round_shared(round_dealt, down_mx[1], down_raw[1], VECTOR_COLS_DOWN)
+        quantise(down_mx[1])
+        round_plain(on_scalar, x_mx[1], x_raw[1], block(PACK - 1))
+        round_plain(on_vector, x_mx[1], x_raw[1], block(0))
+        for tb in range(PACK):
+            if tb + 1 < PACK - 1:
+                round_plain(on_vector, x_mx[1], x_raw[1], block(tb + 1))
+            quantise(x_mx[1], block(tb))
+            h_passes(1, tb)
             round_h(on_scalar, tb)
-        for g in range(1, GROUPS):
-            deal_w4_words(g)
-        for i in range(PACK, BANKS):
+        deal_w4_words(1, 0)
+        deal_w4_words(1, 1)
+        for i in range(PACK):
+            w4_pass(i, 1)
+        for i in range(PACK, EARLY_TILES):
             w4_passes(i)
 
-        late_tiles = list(range(BANKS, TILES))
+        late_tiles = list(range(EARLY_TILES, TILES))
 
         def finish_and_refill(g, u):
             finish_pair(g, u)
-            if g < GROUPS - 1:
+            if 0 < g < GROUPS - 1:
                 store_result(g, tile_pairs[u])
+            elif (g, u) == (0, 1):
+                store_result(g)
             pair = 2 * g + u
-            count = 0 if pair == 0 else 2 if pair in DOUBLE_REFILL else 1
+            count = 2 if pair in DOUBLE_REFILL else 1
             for i in late_tiles[:count]:
                 w4_passes(i)
                 late_tiles.remove(i)
@@ -272,9 +281,8 @@ def tile_mix_lowrank_fm_pl_gelu_kernel(
                 quantise_up(g, u)
                 finish_and_refill(g, u)
 
-        quantise(h_mx, col_halves[0])
         round_shared(round_dealt, up_mx[0], up_raw[0], VECTOR_COLS_UP0)
-        quantise(h_mx, col_halves[1])
+        quantise(h_mx)
         finish_group(0)
         round_dealt(on_vector, up_mx[1], up_raw[1])
         finish_group(1)

@@ -44,7 +44,7 @@ def tile_mix_lowrank_fm_pl_gelu_kernel(
         ctx.enter_context(tc.manual_schedule())
 
         def sbuf(name, shape, dtype):
-            return sbuf_pool.tile(shape, dtype, name=name, align_bytes=64)
+            return sbuf_pool.tile(shape, dtype, name=name, align_bytes=256)
 
         def bank(number, shape):
             return psum_pool.tile(shape, F32, name="bank%d" % (number % BANKS))

@@ -29,8 +29,7 @@ BANKS = 8
 
 VECTOR_COLS_DOWN = 368
 VECTOR_COLS_UP0 = 368
-VECTOR_COLS_LAST = 288
-DOUBLE_REFILL = (1, 5)
+VECTOR_COLS_LAST = 272
 EARLY_TILES = 7
 
 
@@ -247,16 +246,19 @@ def tile_mix_lowrank_fm_pl_gelu_kernel(
 
         round_shared(round_dealt, down_mx[1], down_raw[1], VECTOR_COLS_DOWN)
         quantise(down_mx[1])
-        round_plain(on_scalar, x_mx[1], x_raw[1], block(PACK - 1))
+        last_block = PACK - 1
+        round_plain(on_scalar, x_mx[1], x_raw[1], block(last_block))
         round_plain(on_vector, x_mx[1], x_raw[1], block(0))
         for tb in range(PACK):
-            if tb + 1 < PACK - 1:
+            if tb + 1 < last_block:
                 round_plain(on_vector, x_mx[1], x_raw[1], block(tb + 1))
             quantise(x_mx[1], block(tb))
             h_passes(1, tb)
-            round_h(on_scalar, tb)
+            if tb < last_block:
+                round_h(on_scalar, tb)
         deal_w4_words(1, 0)
-        deal_w4_words(1, 1)
+        round_h(on_vector, last_block)
+        quantise(h_mx, col_halves[0])
         for i in range(PACK):
             w4_pass(i, 1)
         for i in range(PACK, EARLY_TILES):
@@ -264,44 +266,53 @@ def tile_mix_lowrank_fm_pl_gelu_kernel(
 
         late_tiles = list(range(EARLY_TILES, TILES))
 
-        def finish_and_refill(g, u):
-            finish_pair(g, u)
-            if 0 < g < GROUPS - 1:
-                store_result(g, tile_pairs[u])
-            elif (g, u) == (0, 1):
-                store_result(g)
-            pair = 2 * g + u
-            count = 2 if pair in DOUBLE_REFILL else 1
+        def refill(count):
             for i in late_tiles[:count]:
                 w4_passes(i)
                 late_tiles.remove(i)
 
-        def finish_group(g):
-            for u in range(2):
-                quantise_up(g, u)
-                finish_and_refill(g, u)
+        def finish(g, u, refills):
+            finish_pair(g, u)
+            if 0 < g < GROUPS - 1:
+                store_result(g, tile_pairs[u])
+            refill(refills)
 
+        quarters = [block(u) for u in range(PACK)]
         round_shared(round_dealt, up_mx[0], up_raw[0], VECTOR_COLS_UP0)
-        quantise(h_mx)
-        finish_group(0)
+        quantise(h_mx, col_halves[1])
+        quantise_up(0, 0)
+        finish(0, 0, 0)
+        quantise_up(0, 1)
+        deal_w4_words(1, 1)
+        finish(0, 1, 3)
+        store_result(0)
         round_dealt(on_vector, up_mx[1], up_raw[1])
-        finish_group(1)
+        for u in range(2):
+            quantise_up(1, u)
+            finish(1, u, 1)
         round_dealt(on_vector, up_mx[2], up_raw[2])
-        round_plain(on_vector, result_mx[0], result[0], col_halves[0])
-        finish_group(2)
-        round_plain(on_vector, result_mx[0], result[0], col_halves[1])
+        round_plain(on_vector, result_mx[0], result[0], quarters[0])
+        for u in range(2):
+            quantise_up(2, u)
+            finish(2, u, 1 + u)
+        round_plain(on_vector, result_mx[0], result[0], quarters[1])
         round_dealt(on_vector, up_mx[3], up_raw[3])
+        round_plain(on_vector, result_mx[0], result[0], col_halves[1])
+        quantise_up(3, 0)
+        finish(3, 0, 1)
         quantise(result_mx[0])
-        finish_group(3)
+        quantise_up(3, 1)
+        finish(3, 1, 0)
         round_plain(on_vector, result_mx[1], result[1])
         store_words(slice(0, 1))
         for u in range(2):
             store_result(3, tile_pairs[u])
         round_plain(on_vector, result_mx[2], result[2])
         quantise(result_mx[1])
+        store_words(slice(1, 2))
         round_shared(round_plain, result_mx[3], result[3], VECTOR_COLS_LAST)
         quantise(result_mx[2])
-        store_words(slice(1, 3))
+        store_words(slice(2, 3))
         quantise(result_mx[3])
         store_words(slice(3, 4))
         for q in range(P // QUADRANT):

@@ -27,9 +27,10 @@ TILES = M // P
 BIAS_ROW = 8
 BANKS = 8
 
-VECTOR_COLS_DOWN = 368
-VECTOR_COLS_UP0 = 368
-VECTOR_COLS_LAST = 272
+VECTOR_COLS_DOWN = 336
+VECTOR_COLS_UP0 = 448
+VECTOR_COLS_WAIT = 416
+VECTOR_COLS_LAST = 320
 EARLY_TILES = 7
 
 
@@ -199,8 +200,8 @@ def tile_mix_lowrank_fm_pl_gelu_kernel(
             for g in range(GROUPS)
         ]
 
-        def finish_pair(g, u):
-            for s in range(2 * u, 2 * u + 2):
+        def finish_tiles(g, tiles):
+            for s in range(tiles.start, tiles.stop):
                 i = PACK * g + s
                 nc.tensor.matmul_mx(
                     out=y_psum[i][:],
@@ -217,10 +218,10 @@ def tile_mix_lowrank_fm_pl_gelu_kernel(
             rows = out_0[span(g), :].rearrange("(p s) t -> p s t", s=PACK)
             nc.sync.dma_start(out=rows[:, tiles, :], in_=result[g][:, tiles, :])
 
-        def store_words(groups):
+        def store_words(groups, cols=span(0)):
             nc.sync.dma_start(
-                out=out_1[groups].rearrange("g p t i -> p g (t i)").bitcast(I32),
-                in_=result_words[:, groups, :].bitcast(I32),
+                out=out_1[groups, :, cols, :].rearrange("g p t i -> p g (t i)").bitcast(I32),
+                in_=result_words[:, groups, cols].bitcast(I32),
             )
 
         def quantise_up(g, u):
@@ -254,67 +255,68 @@ def tile_mix_lowrank_fm_pl_gelu_kernel(
                 round_plain(on_vector, x_mx[1], x_raw[1], block(tb + 1))
             quantise(x_mx[1], block(tb))
             h_passes(1, tb)
-            if tb < last_block:
-                round_h(on_scalar, tb)
+            round_h(on_scalar, tb)
         deal_w4_words(1, 0)
-        round_h(on_vector, last_block)
-        quantise(h_mx, col_halves[0])
+        deal_w4_words(1, 1)
         for i in range(PACK):
             w4_pass(i, 1)
         for i in range(PACK, EARLY_TILES):
             w4_passes(i)
 
-        late_tiles = list(range(EARLY_TILES, TILES))
+        late_passes = [(i, a) for i in range(EARLY_TILES, TILES) for a in range(K_PASSES)]
 
-        def refill(count):
-            for i in late_tiles[:count]:
-                w4_passes(i)
-                late_tiles.remove(i)
+        def finish(g, tiles):
+            for s in range(tiles.start, tiles.stop):
+                finish_tiles(g, slice(s, s + 1))
+                for i, a in late_passes[: 2 if s == PACK - 1 else 1]:
+                    w4_pass(i, a)
+                    late_passes.remove((i, a))
+            if g < GROUPS - 1:
+                store_result(g, tiles)
 
-        def finish(g, u, refills):
-            finish_pair(g, u)
-            if 0 < g < GROUPS - 1:
-                store_result(g, tile_pairs[u])
-            refill(refills)
+        def split(cols):
+            return slice(0, cols), slice(cols, SPAN)
 
-        quarters = [block(u) for u in range(PACK)]
+        def finish_group(g):
+            for u in range(2):
+                finish(g, tile_pairs[u])
+
         round_shared(round_dealt, up_mx[0], up_raw[0], VECTOR_COLS_UP0)
-        quantise(h_mx, col_halves[1])
+        quantise(h_mx)
         quantise_up(0, 0)
-        finish(0, 0, 0)
         quantise_up(0, 1)
-        deal_w4_words(1, 1)
-        finish(0, 1, 3)
-        store_result(0)
-        round_dealt(on_vector, up_mx[1], up_raw[1])
-        for u in range(2):
-            quantise_up(1, u)
-            finish(1, u, 1)
+        round_shared(round_dealt, up_mx[1], up_raw[1], VECTOR_COLS_WAIT)
+        finish_group(0)
+        quantise_up(1, 0)
+        quantise_up(1, 1)
         round_dealt(on_vector, up_mx[2], up_raw[2])
-        round_plain(on_vector, result_mx[0], result[0], quarters[0])
-        for u in range(2):
-            quantise_up(2, u)
-            finish(2, u, 1 + u)
-        round_plain(on_vector, result_mx[0], result[0], quarters[1])
+        finish_group(1)
+        round_plain(on_vector, result_mx[0], result[0], block(0))
+        quantise_up(2, 0)
+        quantise_up(2, 1)
+        finish_group(2)
+        round_plain(on_scalar, result_mx[1], result[1], split(VECTOR_COLS_WAIT)[1])
         round_dealt(on_vector, up_mx[3], up_raw[3])
-        round_plain(on_vector, result_mx[0], result[0], col_halves[1])
+        round_plain(on_vector, result_mx[0], result[0], split(P)[1])
         quantise_up(3, 0)
-        finish(3, 0, 1)
+        finish(3, tile_pairs[0])
         quantise(result_mx[0])
         quantise_up(3, 1)
-        finish(3, 1, 0)
-        round_plain(on_vector, result_mx[1], result[1])
+        finish(3, tile_pairs[1])
+        round_plain(on_vector, result_mx[1], result[1], split(VECTOR_COLS_WAIT)[0])
         store_words(slice(0, 1))
         for u in range(2):
             store_result(3, tile_pairs[u])
         round_plain(on_vector, result_mx[2], result[2])
         quantise(result_mx[1])
-        store_words(slice(1, 2))
-        round_shared(round_plain, result_mx[3], result[3], VECTOR_COLS_LAST)
         quantise(result_mx[2])
-        store_words(slice(2, 3))
-        quantise(result_mx[3])
-        store_words(slice(3, 4))
+        store_words(slice(1, 3))
+        round_plain(on_scalar, result_mx[3], result[3], split(VECTOR_COLS_LAST)[1])
+        round_plain(on_vector, result_mx[3], result[3], col_halves[0])
+        round_plain(on_vector, result_mx[3], result[3], slice(SPAN // 2, VECTOR_COLS_LAST))
+        for u in range(2):
+            quantise(result_mx[3], col_halves[u])
+            store_words(slice(3, 4), col_halves[u])
         for q in range(P // QUADRANT):
             nc.scalar.dma_start(
                 out=out_2[:, PACK * q : PACK * (q + 1), :].bitcast(I32),

@@ -28,9 +28,8 @@ BIAS_ROW = 8
 BANKS = 8
 
 VECTOR_COLS_DOWN = 336
-VECTOR_COLS_UP0 = 448
-VECTOR_COLS_WAIT = 416
-VECTOR_COLS_LAST = 320
+VECTOR_COLS_UP0 = 416
+VECTOR_COLS_LAST = 304
 EARLY_TILES = 7
 
 
@@ -237,13 +236,15 @@ def tile_mix_lowrank_fm_pl_gelu_kernel(
         bias = sbuf("bias", [P, PACK, GROUPS], F32)
         on_scalar(out=bias[:], in_=bias_psum[:, :, BIAS_ROW:P:QUADRANT])
         quantise(x_mx[0])
-        for i in range(PACK):
+        for i in range(2):
             w4_pass(i, 0)
         round_shared(round_dealt, down_mx[0], down_raw[0], VECTOR_COLS_DOWN)
         deal_w4_words(0, 1)
         quantise(down_mx[0])
         for tb in range(PACK):
             h_passes(0, tb)
+        for i in range(2, PACK):
+            w4_pass(i, 0)
 
         round_shared(round_dealt, down_mx[1], down_raw[1], VECTOR_COLS_DOWN)
         quantise(down_mx[1])
@@ -258,6 +259,7 @@ def tile_mix_lowrank_fm_pl_gelu_kernel(
             round_h(on_scalar, tb)
         deal_w4_words(1, 0)
         deal_w4_words(1, 1)
+        quantise(h_mx, col_halves[0])
         for i in range(PACK):
             w4_pass(i, 1)
         for i in range(PACK, EARLY_TILES):
@@ -282,28 +284,31 @@ def tile_mix_lowrank_fm_pl_gelu_kernel(
                 finish(g, tile_pairs[u])
 
         round_shared(round_dealt, up_mx[0], up_raw[0], VECTOR_COLS_UP0)
-        quantise(h_mx)
-        quantise_up(0, 0)
+        quantise(h_mx, col_halves[1])
+        for s in range(2):
+            quantise(up_mx[0], block(s))
         quantise_up(0, 1)
-        round_shared(round_dealt, up_mx[1], up_raw[1], VECTOR_COLS_WAIT)
+        round_dealt(on_vector, up_mx[1], up_raw[1])
         finish_group(0)
-        quantise_up(1, 0)
+        for s in range(2):
+            quantise(up_mx[1], block(s))
         quantise_up(1, 1)
         round_dealt(on_vector, up_mx[2], up_raw[2])
         finish_group(1)
         round_plain(on_vector, result_mx[0], result[0], block(0))
-        quantise_up(2, 0)
+        for s in range(2):
+            quantise(up_mx[2], block(s))
         quantise_up(2, 1)
         finish_group(2)
-        round_plain(on_scalar, result_mx[1], result[1], split(VECTOR_COLS_WAIT)[1])
         round_dealt(on_vector, up_mx[3], up_raw[3])
         round_plain(on_vector, result_mx[0], result[0], split(P)[1])
-        quantise_up(3, 0)
+        for s in range(2):
+            quantise(up_mx[3], block(s))
         finish(3, tile_pairs[0])
         quantise(result_mx[0])
         quantise_up(3, 1)
         finish(3, tile_pairs[1])
-        round_plain(on_vector, result_mx[1], result[1], split(VECTOR_COLS_WAIT)[0])
+        round_plain(on_vector, result_mx[1], result[1])
         store_words(slice(0, 1))
         for u in range(2):
             store_result(3, tile_pairs[u])

from contextlib import ExitStack

import concourse.mybir as mybir
from concourse.masks import make_identity

K, R, M, T = 1024, 512, 2048, 512
FLOPS = 2 * T * (K * R + K * M + R * M)

F32 = mybir.dt.float32
BF16 = mybir.dt.bfloat16
I32 = mybir.dt.int32
U32 = mybir.dt.uint32
U16 = mybir.dt.uint16
U8 = mybir.dt.uint8
FP8X4 = mybir.dt.float8_e4m3fn_x4
FP4X4 = mybir.dt.float4_e2m1fn_x4
GELU = mybir.ActivationFunctionType.Gelu_apprx_tanh

P = 128
PACK = 4
SPAN = P * PACK
QUADRANT = 32
FP4_BYTES = 2
K_PASSES = K // SPAN
GROUPS = M // SPAN
TILES = M // P
BIAS_ROW = 8
BANKS = 8

VECTOR_COLS_DOWN = 336
VECTOR_COLS_UP0 = 416
VECTOR_COLS_LAST = 304
EARLY_TILES = 7


def tile_mix_lowrank_fm_pl_gelu_kernel(
    tc, x, w4_words, w4_scales, down, up, b, out_0, out_1, out_2
):
    nc = tc.nc
    with ExitStack() as ctx:
        sbuf_pool = ctx.enter_context(tc.tile_pool(name="sbuf", bufs=1))
        psum_pool = ctx.enter_context(tc.psum_pool(name="psum", bufs=1))
        ctx.enter_context(tc.manual_schedule())

        def sbuf(name, shape, dtype):
            return sbuf_pool.tile(shape, dtype, name=name, align_bytes=256)

        def bank(number, shape):
            return psum_pool.tile(shape, F32, name="bank%d" % (number % BANKS))

        def part(number, width):
            return slice(number * width, (number + 1) * width)

        def span(number):
            return part(number, SPAN)

        def block(number):
            return part(number, P)

        w4_scales_raw = sbuf("w4_scales_raw", [P, K_PASSES, M], U8)
        nc.vector.memset(w4_scales_raw[:].rearrange("p a n -> p (a n)").bitcast(I32), 0)
        bias_rows = sbuf("bias_rows", [P, SPAN], F32)
        nc.vector.memset(bias_rows[:], 0.0)
        identity = sbuf("identity", [P, P], F32)
        make_identity(nc, identity[:])

        warm = sbuf("warm", [P, 2], F32)
        nc.vector.memset(warm[:, 0:1], 0.0)
        nc.scalar.activation(out=warm[:, 1:2], in_=warm[:, 0:1], func=GELU)

        def load_rows(name, rows):
            raw = sbuf(name, [P, PACK, rows.shape[1]], F32)
            nc.sync.dma_start(out=raw[:], in_=rows.rearrange("(p j) c -> p j c", j=PACK))
            return raw

        def load_w4_words(a):
            raw = sbuf("w4_words_raw%d" % a, [P, FP4_BYTES * M], U8)
            nc.sync.dma_start(out=raw[:].bitcast(I32), in_=w4_words[a].bitcast(I32))
            return raw

        x_raw = [load_rows("x_raw0", x[span(0), :])]
        for r in range(PACK):
            nc.sync.dma_start(
                out=w4_scales_raw[r:P:QUADRANT, :, :].bitcast(I32),
                in_=w4_scales.rearrange("a (q r) n -> r q a n", r=PACK)[r].bitcast(I32),
            )
        nc.sync.dma_start(out=bias_rows[BIAS_ROW:P:QUADRANT, :], in_=b.rearrange("(g c) -> g c", g=GROUPS))
        w4_words_raw = [load_w4_words(0)]
        down_raw = [load_rows("down_raw%d" % a, down[span(a), :]) for a in range(K_PASSES)]
        x_raw.append(load_rows("x_raw1", x[span(1), :]))
        w4_words_raw.append(load_w4_words(1))
        up_raw = [load_rows("up_raw%d" % g, up[:, span(g)])[:] for g in range(GROUPS)]

        def operand(name):
            rounded = sbuf(name + "_rounded", [P, SPAN, PACK], BF16)
            words = sbuf(name + "_words", [P, SPAN], U32)
            scales = sbuf(name + "_scales", [P, SPAN], U8)
            return rounded, words, scales

        x_mx = [operand("x%d" % a) for a in range(K_PASSES)]
        down_mx = [operand("down%d" % a) for a in range(K_PASSES)]
        up_mx = [operand("up%d" % g) for g in range(GROUPS)]
        h_mx = operand("h")

        def round_plain(copy, mx, raw, cols=span(0)):
            copy(
                out=mx[0][:, cols, :].rearrange("p (c i) j -> p c j i", i=PACK),
                in_=raw[:, :, cols].rearrange("p j (c i) -> p c j i", i=PACK),
            )

        def round_dealt(copy, mx, raw, cols=span(0)):
            dealt = mx[0][:].rearrange("p (s m) j -> p m j s", s=PACK)
            copy(
                out=dealt[:, cols.start // PACK : cols.stop // PACK, :, :],
                in_=raw[:, :, cols].rearrange("p j (m s) -> p m j s", s=PACK),
            )

        def round_shared(rounder, mx, raw, vector_cols):
            rounder(nc.scalar.copy, mx, raw, slice(vector_cols, SPAN))
            rounder(nc.vector.tensor_copy, mx, raw, slice(0, vector_cols))

        def quantise(mx, cols=span(0)):
            rounded, words, scales = mx
            nc.vector.quantize_mx(
                out=words[:, cols].bitcast(FP8X4),
                scales=scales[:, cols],
                in_=rounded[:, cols, :].rearrange("p c j -> p (c j)"),
            )

        on_vector = nc.vector.tensor_copy
        on_scalar = nc.scalar.copy
        tile_pairs = [part(u, 2) for u in range(2)]
        col_halves = [part(u, SPAN // 2) for u in range(2)]

        w4_words_dealt = [
            [sbuf("w4_words_dealt%d_%d" % (a, half), [P, 2, SPAN], U16) for half in range(2)] for a in range(K_PASSES)
        ]
        w4_scales_dealt = [sbuf("w4_scales_dealt%d" % g, [P, K_PASSES, SPAN], U8) for g in range(GROUPS)]

        def deal(dealt, raw):
            on_vector(
                out=dealt[:].rearrange("p a (s m) -> p a m s", s=PACK),
                in_=raw.rearrange("p a (m s) -> p a m s", s=PACK),
            )

        def deal_w4_words(a, half):
            columns = w4_words_raw[a][:].bitcast(U16)[:, part(half, 2 * SPAN)]
            deal(w4_words_dealt[a][half], columns.rearrange("p (g c) -> p g c", g=2))

        def deal_w4_scales(g):
            deal(w4_scales_dealt[g], w4_scales_raw[:, :, span(g)])

        h_psum = [bank(PACK + tb, [P, PACK, P]) for tb in range(PACK)]

        def h_passes(a, tb):
            for s in range(PACK):
                nc.tensor.matmul_mx(
                    out=h_psum[tb][:, s, :],
                    lhsT=down_mx[a][1][:, block(s)].bitcast(FP8X4),
                    lhsT_scale=down_mx[a][2][:, block(s)],
                    rhs=x_mx[a][1][:, block(tb)].bitcast(FP8X4),
                    rhs_scale=x_mx[a][2][:, block(tb)],
                    start=(a == 0 and s == 0),
                    stop=(a == K_PASSES - 1 and s == PACK - 1),
                )

        def round_h(copy, tb):
            copy(out=h_mx[0][:, block(tb), :], in_=h_psum[tb][:].rearrange("p s t -> p t s"))

        y_psum = {}

        def w4_pass(i, a):
            g, s = divmod(i, PACK)
            if a == 0:
                y_psum[i] = bank(i, [P, T])
            nc.tensor.matmul_mx(
                out=y_psum[i][:],
                lhsT=w4_words_dealt[a][g // 2][:, g % 2, block(s)].bitcast(FP4X4),
                lhsT_scale=w4_scales_dealt[g][:, a, block(s)],
                rhs=x_mx[a][1][:].bitcast(FP8X4),
                rhs_scale=x_mx[a][2][:],
                start=(a == 0),
                stop=False,
            )

        def w4_passes(i):
            for a in range(K_PASSES):
                w4_pass(i, a)

        result = [sbuf("result%d" % g, [P, PACK, T], F32) for g in range(GROUPS)]
        result_scales = sbuf("result_scales", [P, T], U8)
        result_words = sbuf("result_words", [P, GROUPS, T], U32)
        result_mx = [
            (
                sbuf("result_rounded%d" % g, [P, T, PACK], BF16),
                result_words[:, g, :],
                result_scales[PACK * g : P, :],
            )
            for g in range(GROUPS)
        ]

        def finish_tiles(g, tiles):
            for s in range(tiles.start, tiles.stop):
                i = PACK * g + s
                nc.tensor.matmul_mx(
                    out=y_psum[i][:],
                    lhsT=up_mx[g][1][:, block(s)].bitcast(FP8X4),
                    lhsT_scale=up_mx[g][2][:, block(s)],
                    rhs=h_mx[1][:].bitcast(FP8X4),
                    rhs_scale=h_mx[2][:],
                    start=False,
                    stop=True,
                )
                nc.scalar.activation(out=result[g][:, s, :], in_=y_psum[i][:], func=GELU, bias=bias[:, s, g : g + 1])

        def store_result(g, tiles=slice(0, PACK)):
            rows = out_0[span(g), :].rearrange("(p s) t -> p s t", s=PACK)
            nc.sync.dma_start(out=rows[:, tiles, :], in_=result[g][:, tiles, :])

        def store_words(groups, cols=span(0)):
            nc.sync.dma_start(
                out=out_1[groups, :, cols, :].rearrange("g p t i -> p g (t i)").bitcast(I32),
                in_=result_words[:, groups, cols].bitcast(I32),
            )

        def quantise_up(g, u):
            quantise(up_mx[g], col_halves[u])

        round_plain(on_scalar, x_mx[0], x_raw[0])
        for g in range(GROUPS):
            deal_w4_scales(g)
        deal_w4_words(0, 0)
        bias_psum = bank(0, [P, PACK, P])
        for s in range(PACK):
            nc.tensor.transpose(bias_psum[:, s, :], bias_rows[:, s:SPAN:PACK], identity[:])
        bias = sbuf("bias", [P, PACK, GROUPS], F32)
        on_scalar(out=bias[:], in_=bias_psum[:, :, BIAS_ROW:P:QUADRANT])
        quantise(x_mx[0])
        for i in range(2):
            w4_pass(i, 0)
        round_shared(round_dealt, down_mx[0], down_raw[0], VECTOR_COLS_DOWN)
        deal_w4_words(0, 1)
        quantise(down_mx[0])
        for tb in range(PACK):
            h_passes(0, tb)
        for i in range(2, PACK):
            w4_pass(i, 0)

        round_shared(round_dealt, down_mx[1], down_raw[1], VECTOR_COLS_DOWN)
        quantise(down_mx[1])
        last_block = PACK - 1
        round_plain(on_scalar, x_mx[1], x_raw[1], block(last_block))
        round_plain(on_vector, x_mx[1], x_raw[1], block(0))
        for tb in range(PACK):
            if tb + 1 < last_block:
                round_plain(on_vector, x_mx[1], x_raw[1], block(tb + 1))
            quantise(x_mx[1], block(tb))
            h_passes(1, tb)
            round_h(on_scalar, tb)
        deal_w4_words(1, 0)
        deal_w4_words(1, 1)
        quantise(h_mx, col_halves[0])
        for i in range(PACK):
            w4_pass(i, 1)
        for i in range(PACK, EARLY_TILES):
            w4_passes(i)

        late_passes = [(i, a) for i in range(EARLY_TILES, TILES) for a in range(K_PASSES)]

        def finish(g, tiles):
            for s in range(tiles.start, tiles.stop):
                finish_tiles(g, slice(s, s + 1))
                for i, a in late_passes[: 2 if s == PACK - 1 else 1]:
                    w4_pass(i, a)
                    late_passes.remove((i, a))
            if g < GROUPS - 1:
                store_result(g, tiles)

        def split(cols):
            return slice(0, cols), slice(cols, SPAN)

        def finish_group(g):
            for u in range(2):
                finish(g, tile_pairs[u])

        round_shared(round_dealt, up_mx[0], up_raw[0], VECTOR_COLS_UP0)
        quantise(h_mx, col_halves[1])
        for s in range(2):
            quantise(up_mx[0], block(s))
        quantise_up(0, 1)
        round_dealt(on_vector, up_mx[1], up_raw[1])
        finish_group(0)
        for s in range(2):
            quantise(up_mx[1], block(s))
        quantise_up(1, 1)
        round_dealt(on_vector, up_mx[2], up_raw[2])
        finish_group(1)
        round_plain(on_vector, result_mx[0], result[0], block(0))
        for s in range(2):
            quantise(up_mx[2], block(s))
        quantise_up(2, 1)
        finish_group(2)
        round_dealt(on_vector, up_mx[3], up_raw[3])
        round_plain(on_vector, result_mx[0], result[0], split(P)[1])
        for s in range(2):
            quantise(up_mx[3], block(s))
        finish(3, tile_pairs[0])
        quantise(result_mx[0])
        quantise_up(3, 1)
        finish(3, tile_pairs[1])
        round_plain(on_vector, result_mx[1], result[1])
        store_words(slice(0, 1))
        for u in range(2):
            store_result(3, tile_pairs[u])
        round_plain(on_vector, result_mx[2], result[2])
        quantise(result_mx[1])
        quantise(result_mx[2])
        store_words(slice(1, 3))
        round_plain(on_scalar, result_mx[3], result[3], split(VECTOR_COLS_LAST)[1])
        round_plain(on_vector, result_mx[3], result[3], col_halves[0])
        round_plain(on_vector, result_mx[3], result[3], slice(SPAN // 2, VECTOR_COLS_LAST))
        for u in range(2):
            quantise(result_mx[3], col_halves[u])
            store_words(slice(3, 4), col_halves[u])
        for q in range(P // QUADRANT):
            nc.scalar.dma_start(
                out=out_2[:, PACK * q : PACK * (q + 1), :].bitcast(I32),
                in_=result_scales[QUADRANT * q : QUADRANT * q + GROUPS * PACK, :].bitcast(I32),
            )
